import numpy as np, ml_dtypes
CORES = [2,6,10,14,18,22,26,30]
N = 8
BF = ml_dtypes.bfloat16
V, W, P, CAP, RO = 512, 4096, 1, 32, 2
def mates(rng):
    o = np.argsort(rng.random((8, 16, W)), axis=-1); m = np.zeros((8, 16, W), np.int64)
    np.put_along_axis(m, o[..., 0::2], o[..., 1::2], -1); np.put_along_axis(m, o[..., 1::2], o[..., 0::2], -1)
    return m, o
def cliques(rng, s, who):
    i = 0
    while i < len(who):
        m = int(rng.integers(2, 10)); c = who[i:i + m]; m = len(c); i += m
        if m > 1: s[np.argsort(rng.random((m, 16)), axis=1)[:, :m - 1], c[:, None]] = c[(np.arange(m)[:, None] + 1 + np.arange(m - 1)) % m]
def net(rng):
    m, o = mates(rng); keep = rng.choice(np.array([0.0, 0.1, 0.25, 0.4, 0.6, 1.0]), (8, 1, W))
    s = np.where(rng.random(m.shape) < keep, m, W); twins = []
    for g in range(8):
        i = rng.permutation(W // 2)[:W // 16]; v = o[g, 0, 2 * i]; b = o[g, 0, 2 * i + 1]
        s[g][:, b] = m[g][:, b]; s[g][0, b] = rng.integers(0, W, len(b)); s[g][0, v] = b
        who = rng.permutation(np.setdiff1d(np.arange(W), np.concatenate([v, b])))[:W // 8]
        s[g][:, who] = W; cliques(rng, s[g], who); twins.append((v, b))
    return s, twins
def pack(x, s):
    cut = lambda a: np.ascontiguousarray(a.reshape(8, 16, N, V).transpose(2, 0, 1, 3).reshape(N, 128, V))
    return {"x": cut(x).astype(np.float32).astype(BF), "stars": cut(s).astype(np.int32)}
def same(x, twins):
    for g in range(8): x[g][:, twins[g][0]] = x[g][:, twins[g][1]]
    return x
def setup_inputs(rng):
    s, twins = net(rng)
    return pack(same(rng.integers(0, 256, (8, 16, W)), twins), s)
def full(rng, s, x):
    a = int(rng.integers(0, N)); v = np.concatenate([q * V + rng.permutation(np.arange(0, V, P))[:CAP] for q in range(N)])
    b = rng.permutation(np.setdiff1d(np.arange(a * V, (a + 1) * V), v))[:N * CAP]
    s[0, v] = b; s[10, v] = rng.choice(np.setdiff1d(np.arange(W), np.concatenate([v, b])), len(v))
def far(rng, s, x):
    o = rng.permutation(W); v = o[o % P == 0][:CAP]; rest = o[~np.isin(o, v)]; b = rest[:CAP]; e = rest[CAP:2 * CAP]; i = np.arange(CAP) & 3
    low = rng.integers(1, 16, (16, CAP)); high = rng.integers(240, 253, (16, CAP))
    high[0] += (np.where(i == 2, 3, 1) - np.add.reduce(high - low, axis=0)) & 3
    near = low.copy(); near[1] += 1; near[2] -= (i == 2).astype(np.int64)
    x[:, b] = low; x[:, v] = np.where(i == 3, near, high); x[:, e] = np.where(i == 3, high, near)
    s[rng.integers(0, 16, CAP), v] = b; m = i > 0; s[8, b[m]] = e[m]; s[0, e[m]] = b[m]
    cliques(rng, s, rest[2 * CAP:])
def again(rng, s, x):
    ends = np.array([0, V - 2, V - 1]); o = [q * V + rng.permutation(np.arange(1, V - 2)) for q in range(N)]
    v = [a[a % P == 0][:CAP] for a in o]; rest = [a[~np.isin(a, c)] for a, c in zip(o, v)]
    for q in range(N):
        b = rest[(q + 1) % N][:CAP]; s[rng.integers(0, 16, CAP), v[q]] = b; x[:, b] = x[:, v[q]]
        s[rng.integers(0, 16, 3), q * V + ends] = rest[(q + 2) % N][CAP:CAP + 3]
        cliques(rng, s, rest[q][CAP + 3:])
def setup_inputs_room(rng):
    s = np.full((8, 16, W), W, np.int64); cyc = (CAP, CAP + 1, CAP - 1, 1, 0); rows = np.arange(16)[:, None]
    x = rng.integers(0, 256, (8, 16, W)); kind = rng.permutation(8)
    for g in range(8):
        if kind[g] > 4:
            (full, far, again)[int(kind[g]) - 5](rng, s[g], x[g])
            continue
        talk = np.zeros(W, bool); to = []
        for q in range(N):
            act = rng.permutation(np.arange(0, V, P)); left = 3 * len(act) // 4; pos = 0
            for d in [0] + list(range(1, N)):
                n = min(cyc[(d - 1 + int(kind[g])) % 5], left - pos); v = q * V + act[pos:pos + n]; pos += n
                talk[v] = True; to.append((v, (q + d) % N))
        rest = rng.permutation(np.flatnonzero(~talk)); cliques(rng, s[g], rest)
        for v, a in to:
            n = len(v); b = rng.choice(rest[rest // V == a], n); k = rng.integers(0, 16, n)
            s[g][:, v] = np.where(rows == k, b, np.where((rows > k) & (rng.random((16, n)) < 0.4), rng.integers(0, W, (16, n)), W))
    return pack(x, s)
def setup_inputs_ties(rng):
    m, o = mates(rng); s = np.where(rng.random(m.shape) < rng.choice(np.array([0.1, 0.4, 0.9, 1.0]), (8, 1, W)), m, W)
    n = rng.permutation(np.array([1, 1, 2, 2, 2, 3, 3, 4]))[:, None, None]
    x = rng.integers(0, 252, (8, 16, 1)) + (rng.random((8, 16, W)) * n).astype(np.int64)
    return pack(x, s)
def setup_inputs_alike(rng):
    s, o = mates(rng); kind = rng.permutation(8) & 3
    for g in range(8):
        q = int(rng.integers(0, N))
        if kind[g] == 0: s[g] = rng.choice(np.array([0, V - 1, V, W - 1]), (16, W))
        elif kind[g] == 1: s[g] = rng.integers(q * V, (q + 1) * V, (16, W))
        elif kind[g] == 2: s[g, 1::2] = s[g, 0::2]; s[g, 4] = np.arange(W)
        else: s[g] = np.repeat(s[g, :1], 16, axis=0); s[g][:, q * V:(q + 1) * V] = W
    s = np.where(rng.random(s.shape) < rng.choice(np.array([0.3, 0.6, 0.9]), (8, 1, W)), s, W)
    return pack(rng.integers(0, 256, (8, 16, W)), s)
def setup_inputs_line(rng):
    m, o = mates(rng); s = np.where(rng.random(m.shape) < rng.choice(np.array([0.3, 0.7, 1.0]), (8, 1, W)), m, W)
    p = rng.integers(0, 256, (8, 1, W)); x = np.where(rng.random((8, 16, 1)) < 0.5, p, 255 - p)
    for g in range(8):
        i = np.argsort(p[g, 0] + rng.random(W)).reshape(-1, 64); low = i[:, :32].reshape(-1); high = i[:, 32:].reshape(-1)
        up = rng.random(len(low)) < 0.5; v = np.where(up, low, high); b = np.where(up, high, low)
        s[g, 0, v] = b; s[g, 0, b] = rng.integers(0, W, len(b))
    return pack(x, s)
def setup_inputs_spread(rng):
    s, twins = net(rng)
    x = (np.exp2(8 * rng.random((8, 1, W))) * rng.random((8, 16, W)) * (rng.random((8, 1, W)) > 0.0625)).astype(np.int64)
    return pack(same(np.minimum(x, 255), twins), s)
def check_inputs(d):
    bad = []; v = np.asarray(d["x"]).astype(np.float32)
    if not (np.min(v) >= 0 and np.max(v) <= 255 and np.all(v == np.floor(v))): bad.append("x: whole numbers from 0 to 255")
    if np.min(d["stars"]) < 0 or np.max(d["stars"]) > W: bad.append("range of stars")
    return bad
def judge(pts, e, b, z):
    live = e < W; xz = pts[z]; xb = pts[b]; xe = pts[e]
    ez = np.add.reduce(np.abs(xe - xz[:, None, :]), axis=2); eb = np.add.reduce(np.abs(xe - xb[:, None, :]), axis=2)
    zb = np.add.reduce(np.abs(xz - xb), axis=1)
    block = np.any(live & (ez < zb[:, None]), axis=1)
    new = np.where(live & (ez < eb), W, e); free = new == W
    new[np.arange(len(b)), np.argmax(free, axis=1)] = z
    return np.where((~block & np.any(free, axis=1))[:, None], new, e)
def reference(x, stars):
    pts = np.zeros((8, W + 1, 16), np.int64); st = np.full((8, W + 1, 16), W, np.int64)
    pts[:, :W] = x.astype(np.float32).astype(np.int64).reshape(N, 8, 16, V).transpose(1, 0, 3, 2).reshape(8, W, 16)
    st[:, :W] = stars.astype(np.int64).reshape(N, 8, 16, V).transpose(1, 0, 3, 2).reshape(8, W, 16)
    for t in range(RO):
        act = np.flatnonzero((np.arange(W) % V) % P == t % P); src = act // V; ks = (5 * t + np.arange(16)) & 15
        new = st.copy()
        for g in range(8):
            mine = st[g][act]; b = mine[:, ks]; c = mine[:, (ks + 1) & 15]; sb = st[g][b]
            hasv = np.any(sb == act[:, None, None], axis=2); hasc = np.any(sb == c[:, :, None], axis=2)
            one = (b < W) & ~hasv; two = (b < W) & hasv & (c < W) & ~hasc
            some = np.any(one | two, axis=1); j = np.argmax(one | two, axis=1); i = np.arange(len(act))
            to = b[i, j]; z = np.where(one[i, j], act, c[i, j])
            for a in range(N):
                here = some & (to // V == a)
                ix = np.concatenate([np.flatnonzero(here & (src == q))[:CAP] for q in range(N)])
                ix = ix[np.unique(to[ix], return_index=True)[1]]
                new[g, to[ix]] = judge(pts[g], st[g][to[ix]], to[ix], z[ix])
        st = new
    y = st[:, :W].reshape(8, N, V, 16).transpose(1, 0, 3, 2).reshape(N, 128, V)
    return {"y": np.ascontiguousarray(y).astype(np.float32)}

@@ -1,0 +1,688 @@
+import numpy as np
+from concourse.bass import DstId, RemoteDMATransfer
+from concourse.mybir import AluOpType as ALU
+from concourse.mybir import ActivationFunctionType as ACT
+
+N, V, W, RO = 8, 512, 4096, 2
+H = 2048
+O = 8
+FL = -(H + O)
+BIG = 8192.0
+NONE = W + O + 300
+WW = NONE + 12
+DUM = 1100
+
+F32, BF, F16, I32, U16 = "float32", "bfloat16", "float16", "int32", "uint16"
+SCRATCH = {}
+
+
+def _sb(names, cols, dtype):
+    for nm in names.split():
+        SCRATCH[nm] = ("sbuf", [128] + (cols if isinstance(cols, list) else [cols]), dtype)
+
+
+_sb("SA", [8, 64], I32)
+_sb("SH", [8, 64], F16)
+_sb("L", [8, 4, 16], F16)
+_sb("L2", [4, 8, 16], F16)
+_sb("WN WI", WW, F32)
+_sb("WX", WW, BF)
+_sb("OFF", 512, U16)
+_sb("S", 8192, F32)
+_sb("EQ", 3072, BF)
+_sb("P16 Q16 RB16 U W16", 512, F16)
+_sb("P32", 768, F32)
+_sb("NF NV TWO GE XZB ED FF", 512, BF)
+_sb("RC32 POS VALS SAT VI", 512, F32)
+_sb("CW", DUM + 516, F32)
+_sb("T1 T2 LI T5 T6", 32, I32)
+_sb("T3 T4 DC", 32, F32)
+_sb("OT OB LP LQ LH", 32, U16)
+_sb("TS", 48, F32)
+_sb("Z1 Z2 Z3 SO1 SO2 DJ OH", 16, F32)
+_sb("E1 QM", 16, BF)
+_sb("SO", 16, U16)
+_sb("OE", 256, U16)
+_sb("BB ZB E32 G1 NEW", 256, F32)
+_sb("M0 NFE", 256, BF)
+_sb("XE MM", 4096, BF)
+_sb("PI", 2, I32)
+_sb("C", 32, F32)
+_sb("QD R0 TMP OQ", 128, BF)
+_sb("I32M R1F", 128, F32)
+_sb("J RP RP16 RPB JZ JZ1 JB JE RK0", 144, BF)
+_sb("CB LM", 2048, BF)
+_sb("REP RG ONES", 1024, BF)
+_sb("M", 32 * 128, BF)
+_sb("SEL ONF", 24, F32)
+for _b in range(8):
+    SCRATCH["B%d" % _b] = ("psum", [128, 512], F32)
+SCRATCH["XS"] = ("dram", [8, 128, 64], BF)
+SCRATCH["XR"] = ("dram", [8, 128, 64], BF)
+SCRATCH["YS"] = ("dram", [8, 128, 64], F32)
+SCRATCH["YR"] = ("dram", [8, 128, 64], F32)
+
+SEMAPHORES = (["cv", "ca", "ct", "cg", "sent", "ld", "xs", "x0", "x1", "xa", "ys", "yo"]
+              + ["sa%d" % i for i in range(N)] + ["ya%d" % i for i in range(N)])
+
+MATS = ["I", "BD", "SHF", "IS", "TA0", "TB0", "TC0", "TA1", "TB1", "TC1", "DM", "PERM", "IB", "NBD", "LO1",
+        "NHI", "N0", "N1", "M10", "M11", "M20", "M21", "ZERO", "BDB", "NBDB", "BD4", "NI", "G1", "G2"]
+COLS = ["p", "pd", "pm", "pd16", "wb", "o1", "bb0", "bb1", "bc0", "bc1", "thr", "ini", "sat", "vb",
+        "lp", "lq", "xo", "dc", "dj", "t1", "t2", "t3", "t4"]
+
+
+def plan(src, cores, topo):
+    me = cores[src]
+    others = [(src + d) % N for d in range(1, N)]
+    near = [q for q in others if topo.chip(cores[q]) == topo.chip(me)]
+    far = [q for q in others if q not in near]
+
+    def hops(q):
+        a, b = topo.chip(me), topo.chip(cores[q])
+        return 1 if (topo.mates(a, b) or topo.same_plane(a, b)) else 2
+    far.sort(key=lambda q: -hops(q))
+    out = topo.engines(me, cores[far[0]])
+    first, second = far[:4], far[4:]
+    calls = [[], []]
+    n1, n2 = len(out) // len(first), len(out) // len(second)
+    for i, q in enumerate(first):
+        calls[0].append((q, out[i * n1:(i + 1) * n1]))
+    for i, q in enumerate(second):
+        calls[1].append((q, out[i * n2:(i + 1) * n2]))
+    for i, q in enumerate(near):
+        free = [e for e in topo.engines(me, cores[q]) if e not in out]
+        calls[0].append((q, free[i * n1:(i + 1) * n1]))
+    return calls
+
+
+def rank_program(g, core, T, topo):
+    R = T.rank_of(core)
+    if R is None:
+        return
+    cores = list(T.cores)
+    queue = {"v": g.vector, "a": g.scalar, "t": g.tensor, "g": g, "s": g.sync}
+    csem = {"v": "cv", "a": "ca", "t": "ct", "g": "cg"}
+    ops, hist, total, flat = [], {}, {}, {}
+
+    def A(name, *idx):
+        if name not in SCRATCH:
+            return {"ap": T[name][idx], "reg": []}
+        shape = SCRATCH[name][1]
+        if len(idx) == 0:
+            idx = (slice(None),)
+        if SCRATCH[name][0] == "sbuf":
+            if name not in flat:
+                flat[name] = np.arange(int(np.prod(shape[1:]))).reshape(shape[1:])
+            f = flat[name][idx[1:]] if len(idx) > 1 else flat[name]
+            lo, hi = int(np.min(f)), int(np.max(f)) + 1
+        elif SCRATCH[name][0] == "dram" and isinstance(idx[0], int):
+            lo, hi = idx[0], idx[0] + 1
+        else:
+            lo, hi = 0, 1 << 30
+        return {"ap": T[name][idx], "reg": [(name, lo, hi)]}
+
+    al = slice(None)
+
+    def cs(name, lo, hi, step=1):
+        return A(name, al, slice(lo, hi, step) if step != 1 else slice(lo, hi))
+
+    def ind(win, off):
+        return {"ap": win["ap"].indirect(off["ap"]), "reg": win["reg"], "off": off["reg"]}
+
+    def val(x):
+        return x["ap"] if isinstance(x, dict) else x
+
+    def rec(eng, call, outs, ins, sem=None, inc=16):
+        rd, wr = [], []
+        for x in ins:
+            if isinstance(x, dict):
+                rd += x["reg"] + x.get("off", [])
+        for x in outs:
+            wr += x["reg"]
+            rd += x.get("off", [])
+        me = len(ops)
+        deps = set()
+        for regs, isw in ((rd, False), (wr, True)):
+            for nm, lo, hi in regs:
+                ps = SCRATCH[nm][0] == "psum"
+                for (l2, h2, o2, w2) in hist.get(nm, []):
+                    if l2 < hi and lo < h2:
+                        other = ops[o2]
+                        same = other["eng"] == eng and other["sem"] is None and sem is None
+                        if same and eng == "t":
+                            continue
+                        if sem is not None and other["sem"] == sem:
+                            continue
+                        if isw or w2 or (ps and not same):
+                            deps.add(o2)
+        for regs, isw in ((rd, False), (wr, True)):
+            for nm, lo, hi in regs:
+                h = hist.setdefault(nm, [])
+                if isw and sem is None:
+                    h[:] = [e for e in h if not (lo <= e[0] and e[1] <= hi)]
+                h.append((lo, hi, me, isw))
+        if sem is not None:
+            total[sem] = total.get(sem, 0) + inc
+        ops.append({"eng": eng, "call": call, "deps": deps, "sem": sem, "sig": False, "n": 0})
+
+    def ts(out, in0, s1, op0, s2=None, op1=None):
+        if op1 is None:
+            rec("v", lambda: g.vector.tensor_scalar(val(out), val(in0), val(s1), None, op0), [out], [in0, s1])
+        else:
+            rec("v", lambda: g.vector.tensor_scalar(val(out), val(in0), val(s1), val(s2), op0, op1), [out], [in0, s1, s2])
+
+    def tt(out, a, b, op):
+        rec("v", lambda: g.vector.tensor_tensor(val(out), val(a), val(b), op), [out], [a, b])
+
+    def cp(out, a):
+        rec("v", lambda: g.vector.tensor_copy(val(out), val(a)), [out], [a])
+
+    def ms(out, c):
+        rec("v", lambda: g.vector.memset(val(out), c), [out], [])
+
+    def act(out, a, func, bias=0.0, scale=1.0):
+        rec("a", lambda: g.scalar.activation(val(out), val(a), func, bias=val(bias), scale=val(scale)), [out], [a, bias, scale])
+
+    def mm(out, lhsT, rhs, start=True, stop=True):
+        rec("t", lambda: g.tensor.matmul(val(out), val(lhsT), val(rhs), start, stop), [out], [lhsT, rhs])
+
+    def iota(out, pat, base, cm):
+        fl = SCRATCH[out["reg"][0][0]][2] != I32
+        if fl:
+            rec("g", lambda: g.iota(val(out), pat, base, cm, allow_small_or_imprecise_dtypes=True), [out], [])
+        else:
+            rec("g", lambda: g.iota(val(out), pat, base, cm), [out], [])
+
+    def asel(out, a, pat, op, base, cm, fill=0.0):
+        rec("g", lambda: g.affine_select(val(out), val(a), pat, op, fill, base, cm), [out], [a])
+
+    def dma(eng, out, a, sem):
+        rec(eng, lambda: queue[eng].dma_start(val(out), val(a)).then_inc(T.sem[sem], 16), [out], [a], sem=sem)
+
+    def send(src_of, dst, sem):
+        for call in plan(R, cores, topo):
+            trs, n = [], 0
+            for q, engs in call:
+                rid, pid = topo.addr(cores[q])[:2]
+                trs.append(RemoteDMATransfer(dst_ids=[DstId(rid=rid, pnc=pid)], dma_engine_mask=sum(1 << e for e in engs),
+                                             remote_sem=T.sem[sem], src=src_of(q)["ap"], dst=dst["ap"]))
+                n += len(engs)
+            rec("g", lambda trs=trs: g.remote_dma_fused(trs, local_sem=T.sem["sent"]), [],
+                [src_of(q) for q, _ in call], sem="sent", inc=n)
+
+    def arrive(q, out, sem):
+        n = [len(e) for call in plan(q, cores, topo) for d, e in call if d == R][0]
+        rec("x", None, [out], [], sem=sem, inc=n)
+
+    def M(name):
+        i = MATS.index(name)
+        return cs("M", 128 * i, 128 * i + 128)
+
+    def C(name):
+        i = COLS.index(name)
+        return cs("C", i, i + 1)
+
+    def red(name, k):
+        return cs(name, 15 - k, 143 - k)
+
+    def B(i, lo=0, hi=512, step=1):
+        return cs("B%d" % i, lo, hi, step)
+
+    EQo, NE, GT, GE_, LT = ALU.is_equal, ALU.not_equal, ALU.is_gt, ALU.is_ge, ALU.is_lt
+    ADD, SUB, MUL, MAX, MIN = ALU.add, ALU.subtract, ALU.mult, ALU.max, ALU.min
+    WB = 7
+    WN, WX, WI = A("WN"), A("WX"), A("WI")
+
+    def sel(out, a, ap, ax, ak, d, op, fill=0.0):
+        asel(M(out), M(a), [[ax, 8], [ak, 16]], op, d, ap, fill)
+
+    def diag(out, a, d, fill):
+        sel(out, a, -1, 16, 1, -d, NE, fill)
+
+    def line(out, a, d):
+        sel(out, a, -1, 16, 1, -d, EQo)
+
+    def rows(out, a, lo, hi, fill=0.0):
+        if hi is None:
+            sel(out, a, 1, -16, 0, -lo, GE_, fill)
+        else:
+            sel(out, a, -1, 16, 0, hi, GE_, fill)
+
+    def aff(out, a, scale, bias):
+        act(out, a, ACT.Copy, bias=float(bias), scale=float(scale))
+
+    for q in range(N):
+        dma("s" if q % 2 == 0 else "a", A("SA", al, q), A("stars", slice(16 * q, 16 * q + 16), al), "ld")
+    dma("s", A("XS"), A("x", al), "xs")
+
+    iota(cs("PI", 0, 1), [[0, 1]], 0, 1)
+    iota(A("R0"), [[0, 8], [-8, 16]], 0, 1)
+    iota(A("QD"), [[1, 8], [0, 16]], 0, 0)
+    iota(A("QM"), [[1, 16]], 0, 0)
+    iota(cs("J", 0, 143), [[1, 143]], -15, 0)
+    iota(A("LI"), [[16, 32]], 0, 1)
+    iota(A("VI"), [[1, 512]], 0, 0)
+    ms(cs("WN", 0, O), float(H))
+    ms(cs("WN", W + O, WW), float(H))
+    cp(C("p"), cs("PI", 0, 1))
+    ts(cs("PI", 1, 2), cs("PI", 0, 1), 4, ALU.arith_shift_right)
+    ms(cs("WX", 0, O), 0.0)
+    cp(C("pd"), cs("PI", 1, 2))
+    ms(cs("WX", W + O, WW), 0.0)
+    ts(C("pd16"), C("pd"), 16.0, MUL)
+    ts(M("BD"), A("QD"), C("pd"), EQo)
+    tt(C("pm"), C("p"), C("pd16"), SUB)
+
+    ts(A("SH"), A("SA"), float(-H), ADD)
+    send(lambda q: A("SH", al, q), A("L", al, R), "sa%d" % R)
+    send(lambda q: A("XS", q), A("XR", R), "xa")
+    for b in range(4):
+        ts(A("L", al, R, b), A("SA", al, R, slice(16 * b, 16 * b + 16)), float(-H), ADD)
+    others = [q for q, _ in plan(R, cores, topo)[0][4:]]
+    others += [q for q in range(N) if q != R and q not in others]
+    for q in others:
+        arrive(q, A("L", al, q), "sa%d" % q)
+        arrive(q, A("XR", q), "xa")
+
+    for q in range(N):
+        src = A("x", slice(16 * R, 16 * R + 16), al) if q == R else A("XR", q)
+        dma("s", A("WX", slice(0, 16), slice(O + V * q, O + V * q + V)), src, "x0")
+    for x in range(1, 8):
+        dma("s", A("WX", slice(16 * x, 16 * x + 16), slice(O, O + W)), A("WX", slice(0, 16), slice(O, O + W)), "x1")
+
+    ms(A("ONES"), 1.0)
+    ts(A("OH"), A("QM"), C("pm"), EQo)
+    ts(cs("RP", 0, 143), cs("J", 0, 143), C("pd16"), EQo)
+    for vh in range(8):
+        ts(cs("REP", 128 * vh, 128 * vh + 128), A("R0"), float(vh), EQo)
+    aff(C("wb"), C("pd"), 512, -H)
+    aff(C("lp"), C("pd"), 496, O)
+    aff(C("dc"), C("pd"), -16, DUM)
+    aff(C("dj"), C("pd"), -16, V)
+    aff(C("xo"), C("pd"), -512, -O)
+    aff(C("lq"), C("pd"), 48, O)
+    aff(M("NBD"), M("BD"), -1, 0)
+    aff(M("BDB"), M("BD"), BIG, 0)
+    aff(M("NBDB"), M("BD"), -BIG, 0)
+    aff(C("t1"), C("pm"), 512, O + 16 * FL)
+    aff(C("ini"), C("pm"), 32, 0)
+    aff(C("t2"), C("pm"), 32, 32.5)
+    aff(C("bb0"), C("pm"), -BIG, 0)
+    aff(C("bc0"), C("pm"), -BIG, -BIG - FL)
+    act(B(WB), A("VI"), ACT.Identity, bias=C("wb"))
+    for l in range(16):
+        l = (l + 1) % 16
+        act(cs("CB", 128 * l, 128 * l + 128), M("BD"), ACT.Identity, scale=cs("OH", l, l + 1))
+    aff(M("BD4"), M("BD"), W, 0)
+    aff(cs("RPB", 0, 143), cs("RP", 0, 143), BIG, 0)
+    asel(M("I"), cs("ONES", 0, 128), [[1, 128]], EQo, 0, -1)
+    iota(A("T5"), [[16, 4], [512, 8]], 0, 1)
+    iota(A("T6"), [[1, 2], [2, 8], [0, 2]], 0, 0)
+    iota(A("TMP"), [[0, 8], [1, 16]], -5, 0)
+    for k in range(5):
+        asel(A("OQ" if k % 2 == 0 else "TMP"), A("TMP" if k % 2 == 0 else "OQ"), [[0, 8], [1, 16]], NE, -k, 0, float(k + 11))
+    ts(A("LP"), A("LI"), C("lp"), ADD)
+    ms(cs("CW", 0, 264), float(NONE))
+    ms(M("ZERO"), 0.0)
+    ms(A("ONF"), 1.0)
+    ts(A("W16"), A("VI"), C("wb"), ADD)
+    ts(A("DC"), A("LI"), C("dc"), ADD)
+    ts(A("DJ"), cs("LI", 0, 16), C("dj"), ADD)
+    ts(C("thr"), cs("OH", 15, 16), -1.0e6, MUL, C("t1"), ADD)
+    ts(C("sat"), cs("OH", 15, 16), BIG, MUL, C("t2"), ADD)
+    ts(C("t3"), cs("OH", 0, 1), float(-16 * FL), MUL)
+    ts(C("t4"), C("pm"), 5.0, LT, 16.0, MUL)
+    ts(C("vb"), cs("OH", 2, 3), float(-FL), MUL, C("t3"), ADD)
+    ts(C("o1"), C("t4"), C("pm"), ADD, -5.0, ADD)
+    cp(cs("JZ1", 0, 8), cs("RP", 0, 8))
+    tt(cs("JZ1", 8, 143), cs("RP", 8, 143), cs("RP", 0, 135), ADD)
+    ts(A("LQ"), A("T5"), C("lq"), ADD)
+    cp(A("LH"), A("T6"))
+    ts(A("QD"), A("OQ"), C("o1"), GT, BIG, MUL)
+    tt(M("TC1"), A("QD"), M("BD"), MUL)
+    line("G1", "BD", -1)
+    sel("SHF", "G1", 16, -256, -1, 15, NE, 1.0)
+    diag("IS", "SHF", 0, 1.0)
+    sel("TC0", "BDB", -1, 16, 1, 0, GT)
+    diag("TA0", "TC0", 0, -BIG)
+    sel("G1", "NBDB", -1, 16, 1, 0, GT)
+    diag("TB0", "G1", 0, BIG)
+    line("G2", "NBD", -1)
+    sel("G1", "G2", 16, -256, -1, 15, NE, -1.0)
+    diag("G2", "G1", 0, 1.0)
+    sel("DM", "G2", 0, 0, 1, -14, NE)
+    asel(A("SEL"), A("ONF"), [[-1, 3], [-16, 8]], EQo, 0, 1)
+    line("IB", "BDB", 0)
+    sel("LO1", "BD", 0, 0, -1, 8, GT)
+    sel("NHI", "NBD", 0, 0, 1, -8, GE_)
+    line("NI", "NBD", 0)
+    diag("G1", "IB", 8, BIG)
+    rows("G2", "G1", 0, None)
+    rows("N0", "G2", None, 7)
+    diag("G1", "IB", -8, BIG)
+    rows("G2", "G1", 8, None)
+    rows("N1", "G2", None, 15)
+    for nm, d in (("M10", 0), ("M11", 8)):
+        line("G1", "BD4", d)
+        rows("G2", "G1", None, 7, -BIG)
+        rows(nm, "G2", None, 15)
+    rows("G1", "TA0", None, 7, BIG)
+    rows("M20", "G1", None, 15)
+    sel("G1", "BDB", -1, 16, 1, -8, GT)
+    diag("G2", "G1", 8, -BIG)
+    rows("G1", "G2", 0, None)
+    rows("G2", "G1", None, 7, BIG)
+    rows("M21", "G2", None, 15)
+    diag("TA1", "TC1", 0, -BIG)
+    for s in range(16):
+        asel(cs("LM", 128 * s, 128 * s + 128), red("RPB", s), [[1, 128]], GT, 0, -1)
+    iota(cs("WI", H, WW), [[1, WW - H]], H, 0)
+    asel(A("RG"), A("ONES"), [[-16, 8], [0, 8], [-1, 16]], EQo, 0, 1)
+    asel(M("PERM"), cs("ONES", 0, 128), [[-1, 16], [-16, 8]], EQo, 0, 1)
+
+    def wcopy(i, q, bank):
+        dst = cs("WN", O + V * q, O + V * q + V)
+        if i % 2 == 0:
+            act(dst, B(bank), ACT.Copy)
+        else:
+            cp(dst, B(bank))
+
+    for t in range(RO):
+        if t == 0:
+            order = [R] + others
+            for i, q in enumerate(order):
+                bank = (2, 3, 4, 6)[i % 4]
+                cp(A("L2", al, al, q), A("L", al, q))
+                for vh in range(8):
+                    mm(B(bank, 64 * vh, 64 * vh + 64), cs("REP", 128 * vh, 128 * vh + 128), A("L", al, q))
+                if i == N - 1:
+                    for b in range(4):
+                        mm(B(5, b, 512, 4), A("L2", al, b), M("I"))
+                    ts(A("OFF"), B(5), float(-FL), ADD)
+                wcopy(i + 1, q, bank)
+            cp(A("P16"), ind(WN, A("LP")))
+            ts(A("NF"), A("P16"), float(H), EQo)
+        else:
+            ts(A("P16"), cs("P32", 0, V), float(-H), ADD)
+            for q in range(N):
+                bank = (2, 3, 4, 6)[q % 4]
+                mm(B(bank), cs("RG", 128 * q, 128 * q + 128), A("P16"))
+                wcopy(q, q, bank)
+                if q >= 4:
+                    for s in range(4 * q - 16, 4 * q - 12):
+                        mm(B(1, 0, 32), red("RK0", s), cs("P16", s, V, 16), s == 0, s == 15)
+            ts(cs("OFF", 0, 32), B(1, 0, 32), float(-FL), ADD)
+            cp(A("Q16"), ind(WN, A("LQ")))
+            for b in range(4):
+                mm(B(5, b, 512, 4), cs("Q16", 128 * b, 128 * b + 128), M("PERM"))
+
+        def Sk(k):
+            return cs("S", V * k, V * k + V)
+
+        def eqt(k, c):
+            i = 2 * (k % 3) + c
+            return cs("EQ", V * i, V * i + V)
+
+        def cb(k):
+            l = (k + 1) % 16
+            mm(B(2 + k % 3), cs("CB", 128 * l, 128 * l + 128), A("P16"))
+
+        def eqw(k):
+            tt(eqt(k, 0), Sk(k), B(WB), EQo)
+            mm(B(0), red("RP", k), eqt(k, 0), k == 0, k == 15)
+            if k == 8:
+                mm(B(0), M("I"), A("NF"), False, False)
+
+        def eqc(k):
+            tt(eqt(k, 1), Sk(k), B(2 + k % 3), EQo)
+            mm(B(1), red("RP", k), eqt(k, 1), k == 0, k == 15)
+            if k == 8:
+                mm(B(1), M("IS"), A("NF"), False, False)
+            if k + 3 < 16:
+                cb(k + 3)
+
+        def gather(k):
+            act(Sk(k), ind(WN, cs("OFF", 32 * k, 32 * k + 32)), ACT.Copy)
+
+        gather(0)
+        if t > 0:
+            act(A("NF"), cs("P32", 0, V), ACT.Relu, bias=float(1 - W))
+        for k in range(3):
+            cb(k)
+        if t > 0:
+            ts(cs("OFF", 32, 96), B(5, 32, 96), float(-FL), ADD)
+        eqw(0)
+        if t > 0:
+            ts(cs("OFF", 96, V), B(5, 96, V), float(-FL), ADD)
+        for k in range(1, 16):
+            gather(k)
+        if t == 0:
+            aff(cs("RP16", 0, 143), cs("RP", 0, 143), 1.0 / 16, 0)
+            aff(A("R1F"), red("RP", 1), 1, 0)
+            act(A("SAT"), A("VI"), ACT.Identity, bias=C("sat"), scale=0.0)
+            act(cs("P32", 0, V), ind(WN, A("LP")), ACT.Copy, bias=float(H))
+        eqc(0)
+        for k in range(1, 13):
+            eqw(k)
+            eqc(k)
+        eqw(13)
+        eqw(14)
+        eqw(15)
+        act(A("NV"), B(0), ACT.Sign)
+        if t == 0:
+            aff(cs("WI", 0, V), A("VI"), 1, 0)
+        hs = [(0, 256), (256, 512)]
+        for h, (lo, hi) in enumerate(hs):
+            mm(B(5 + h, 0, 256), M("I"), cs("P16", lo, hi), True, False)
+        eqc(13)
+        mm(B(3), M("SHF"), A("P16"), True, False)
+        eqc(14)
+        for h, (lo, hi) in enumerate(hs):
+            mm(B(5 + h, 0, 256), M("TA%d" % t), cs("NV", lo, hi), False, False)
+        eqc(15)
+
+        mm(B(3), M("TC%d" % t), A("NV"), False, False)
+        for h, (lo, hi) in enumerate(hs):
+            tt(cs("TWO", lo, hi), B(1, lo, hi), cs("NV", lo, hi), LT)
+            mm(B(5 + h, 0, 256), M("TB%d" % t), cs("TWO", lo, hi), False, True)
+        mm(B(3), M("TB%d" % t), A("TWO"), False, True)
+        act(A("RC32"), B(3), ACT.Relu, bias=C("bc%d" % t))
+        for h, (lo, hi) in enumerate(hs):
+            ts(cs("RB16", lo, hi), B(5 + h, 0, 256), C("bb%d" % t), ADD, float(FL), MAX)
+            mm(B(2 + 2 * h, 0, 256), M("BD"), cs("RB16", lo, hi))
+        mm(B(0), red("RP16", 2), A("W16"), True, False)
+        for h, (lo, hi) in enumerate(hs):
+            ts(cs("GE", lo, hi), B(2 + 2 * h, 0, 256), C("thr"), GE_)
+            mm(B(5 + h, 0, 256), M("DM"), cs("GE", lo, hi))
+            if h == 0:
+                mm(B(0), red("RP", 0), A("RB16"), False, False)
+        mm(B(0), A("R1F"), A("RC32"), False, True)
+        if t == 0:
+            aff(cs("WI", V, 2 * V), A("VI"), 1, V)
+        act(A("VALS"), B(0), ACT.Identity, bias=C("vb"))
+        if t == 0:
+            for i in (2, 3):
+                aff(cs("WI", i * V, i * V + V), A("VI"), 1, i * V)
+            aff(cs("JB", 0, 143), cs("RP", 0, 143), -2, 0)
+            aff(cs("JE", 0, 143), cs("RP", 0, 143), -1, 0)
+            aff(cs("JZ", 0, 143), cs("JZ1", 0, 143), 2, 0)
+            aff(A("I32M"), M("I"), 1, 0)
+            aff(M("TB1"), M("TA1"), -1, 0)
+            act(cs("RK0", 0, 143), cs("RP", 0, 143), ACT.Identity, scale=cs("OH", 0, 1))
+            aff(C("bb1"), C("o1"), -BIG, 0)
+            aff(C("bc1"), C("o1"), -BIG, -BIG - FL)
+        for h, (lo, hi) in enumerate(hs):
+            ini = C("ini") if h == 0 else cs("POS", lo - 1, lo)
+            pos, src, sat = cs("POS", lo, hi), B(5 + h, 0, 256), cs("SAT", lo, hi)
+            rec("v", lambda pos=pos, src=src, sat=sat, ini=ini: g.vector.tensor_tensor_scan(
+                val(pos), val(src), val(sat), val(ini), ADD, MIN), [pos], [src, sat, ini])
+        for h, (lo, hi) in enumerate(hs):
+            tt(cs("U", lo, hi), cs("POS", lo, hi), B(5 + h, 0, 256), MUL)
+        for s in range(16):
+            mm(B(2, 0, 32), red("RP", s), cs("U", s, V, 16), s == 0, s == 15)
+        ts(A("T1"), B(2, 0, 32), 2.0, MUL)
+        ts(A("T2"), A("T1"), 1, ALU.bitwise_and)
+        tt(A("T3"), A("T2"), A("DC"), MUL)
+        tt(A("T4"), B(2, 0, 32), A("T3"), MAX)
+        cp(A("OT"), A("T4"))
+        cp(ind(A("CW"), A("OT")), A("VALS"))
+        for h in range(2):
+            mm(B(1, h, 48, 2), cs("CW", 1 + h, 257 + h, 2), A("SEL"))
+
+        OBZ, OBB = cs("OB", 0, 16), cs("OB", 16, 32)
+        pat = {1: 2, 0: 4}
+        acc = {1: 6, 0: 0}
+        cnt = [0]
+
+        def xzb(c, z):
+            return cs("XZB", 256 * z + 128 * c, 256 * z + 128 * c + 128)
+
+        def obs(c, z):
+            return cs("OB", 16 * z + 8 * c, 16 * z + 8 * c + 8)
+
+        def patterns(c):
+            for z in range(2):
+                for i in range(4):
+                    mm(B(pat[c] + z, i, 512, 4), M("I"), xzb(c, z))
+
+        def unit(c, q):
+            lo, hi = 2048 * c, 2048 * c + 2048
+            regs = [B(acc[c], 128 * (j // 2), 128 * (j // 2) + 128) for j in range(4)]
+            for j in range(4):
+                mm(regs[j], red("JE", 8 + (q + 4 * j) % 8), cs("XE", lo + q + 4 * j, hi, 16), False, False)
+            for z in range(2):
+                m0 = V * (cnt[0] % 8)
+                cnt[0] += 1
+                tt(cs("MM", m0, m0 + V), cs("XE", lo + q, hi, 4), B(pat[c] + z), MAX)
+                for j in range(4):
+                    mm(regs[j], red("JB" if z else "JZ", (q + 4 * j) % 8), cs("MM", m0 + j, m0 + V, 4), False,
+                       q == 3 and z == 1 and j == 3)
+
+        def terms(c):
+            for ih in range(2):
+                reg = B(acc[c], 128 * ih, 128 * ih + 128)
+                mm(reg, M("NBD"), xzb(c, 0), False, False)
+                mm(reg, M("LO1"), xzb(c, 1), False, False)
+                mm(reg, M("NHI"), cs("M0", 128 * c, 128 * c + 128), False, False)
+                mm(reg, M("N%d" % ih), cs("NFE", 128 * c, 128 * c + 128), False, False)
+
+        def early(c, qb):
+            lo = 128 * c
+            mm(B(qb, 0, 128), A("I32M"), cs("ZB", lo, lo + 128), True, False)
+            mm(B(qb, 0, 128), M("TA0"), cs("NFE", lo, lo + 128), False, False)
+
+        def flags(c, qb):
+            lo = 128 * c
+            ts(cs("FF", 2 * lo, 2 * lo + 256), B(acc[c], 0, 256), 0.0, LT)
+            for ih in range(2):
+                mm(B(qb, 0, 128), M("M2%d" % ih), cs("FF", 2 * lo + 128 * ih, 2 * lo + 128 * ih + 128), False, ih == 1)
+            for ih in range(2):
+                mm(B(qb, 128, 256), M("M1%d" % ih), cs("FF", 2 * lo + 128 * ih, 2 * lo + 128 * ih + 128), ih == 0, ih == 1)
+
+        def new(c, qb):
+            lo = 128 * c
+            tt(cs("G1", lo, lo + 128), cs("E32", lo, lo + 128), B(qb, 128, 256), MAX)
+            tt(cs("NEW", lo, lo + 128), cs("G1", lo, lo + 128), B(qb, 0, 128), MIN)
+
+        def write(q):
+            cp(ind(A("P32"), cs("SO", 2 * q, 2 * q + 2)), cs("NEW", 32 * q, 32 * q + 32))
+
+        cp(OBB, B(1, 0, 16))
+        ts(A("OE"), ind(WN, OBB), float(-FL), ADD)
+        act(A("BB"), ind(WI, OBB), ACT.Copy)
+        act(cs("XE", 2048, 3840), ind(WX, cs("OE", 128, 240)), ACT.Copy)
+        cp(A("TS"), B(1, 0, 48))
+        BW = cs("TS", 0, 16)
+        ts(A("Z1"), cs("TS", 16, 32), 0.0, EQo)
+        tt(cs("E1", 0, 8), cs("TS", 0, 16, 2), cs("TS", 1, 16, 2), EQo)
+        tt(A("Z2"), A("Z1"), cs("TS", 32, 48), MUL)
+        tt(A("Z3"), A("Z2"), cs("TS", 16, 32), ADD)
+        cp(OBZ, A("Z3"))
+        for z in range(2):
+            cp(xzb(1, z), ind(WX, obs(1, z)))
+        patterns(1)
+        for z in range(2):
+            act(xzb(0, z), ind(WX, obs(0, z)), ACT.Copy)
+        act(cs("XE", 0, 2048), ind(WX, cs("OE", 0, 128)), ACT.Copy)
+        cp(cs("XE", 3840, 4096), ind(WX, cs("OE", 240, 256)))
+        for h in range(2):
+            tt(cs("ED", 256 * h, 256 * h + 256), ind(BW, cs("LH", 16 * h, 16 * h + 16)), A("BB"), EQo)
+        mm(B(acc[1], 0, 256), M("ZERO"), cs("NF", 0, 256), True, False)
+        mm(B(1, 0, 32), M("ZERO"), cs("NF", 0, 32), True, False)
+        mm(B(1, 0, 16), A("I32M"), BW, False, False)
+        mm(B(1, 1, 16, 2), M("IB"), cs("E1", 0, 8), False, False)
+        for s in range(16):
+            mm(B(1, 0, 32), cs("LM", 128 * s, 128 * s + 128), cs("ED", s, V, 16), False, s == 15)
+        act(A("E32"), ind(WN, OBB), ACT.Copy, bias=float(H))
+        act(A("NFE"), A("E32"), ACT.Relu, bias=float(1 - W))
+        unit(1, 0)
+        ts(A("SO1"), B(1, 0, 16), C("xo"), ADD)
+        tt(A("SO2"), B(1, 16, 32), A("SO1"), ADD)
+        patterns(0)
+        unit(1, 1)
+        tt(A("SO1"), A("SO2"), A("DJ"), MIN)
+        mm(B(1, 0, 256), M("I"), cs("XZB", 0, 256), True, False)
+        mm(B(1, 0, 256), M("NI"), cs("XZB", 256, 512), False, True)
+        act(A("M0"), B(1, 0, 256), ACT.Abs)
+        act(A("ZB"), ind(WI, OBZ), ACT.Copy, bias=BIG - O)
+        if t == 0:
+            aff(cs("CW", 0, 264), cs("VI", 0, 264), 0, NONE)
+        unit(1, 2)
+        cp(A("SO"), A("SO1"))
+        mm(B(acc[0], 0, 256), M("ZERO"), cs("NF", 0, 256), True, False)
+        terms(1)
+        unit(1, 3)
+        early(1, 1)
+        unit(0, 0)
+        terms(0)
+        unit(0, 1)
+        flags(1, 1)
+        early(0, 2)
+        unit(0, 2)
+        new(1, 1)
+        unit(0, 3)
+        write(7)
+        write(6)
+        flags(0, 2)
+        write(5)
+        write(4)
+        new(0, 2)
+        for q in (3, 2, 1, 0):
+            write(q)
+
+    dma("s", A("YS"), cs("P32", 0, V), "ys")
+    dma("a", A("y", slice(16 * R, 16 * R + 16), al), A("P32", slice(16 * R, 16 * R + 16), slice(0, V)), "yo")
+    send(lambda q: A("YS", q), A("YR", R), "ya%d" % R)
+    for i, q in enumerate(others):
+        arrive(q, A("YR", q), "ya%d" % q)
+        dma("s" if i % 2 == 0 else "a", A("y", slice(16 * q, 16 * q + 16), al), A("YR", q), "yo")
+
+    for o in ops:
+        for d in o["deps"]:
+            ops[d]["sig"] = True
+    done = {}
+    for o in ops:
+        if o["sem"] is None and o["sig"]:
+            done[o["eng"]] = done.get(o["eng"], 0) + 1
+            o["n"] = done[o["eng"]]
+    seen = {}
+    for o in ops:
+        if o["eng"] == "x":
+            continue
+        need = {}
+        for d in o["deps"]:
+            p = ops[d]
+            s, v = (p["sem"], total[p["sem"]]) if p["sem"] is not None else (csem[p["eng"]], p["n"])
+            need[s] = max(need.get(s, 0), v)
+        for s in sorted(need):
+            if seen.get((o["eng"], s), 0) < need[s]:
+                queue[o["eng"]].wait_ge(T.sem[s], need[s])
+                seen[(o["eng"], s)] = need[s]
+        r = o["call"]()
+        if o["sem"] is None and o["sig"]:
+            r.then_inc(T.sem[csem[o["eng"]]], 1)
+    for e in done:
+        total[csem[e]] = done[e]
+    for s in sorted(total):
+        if max([seen.get((e, s), 0) for e in queue]) < total[s]:
+            g.wait_ge(T.sem[s], total[s])

@@ -10,7 +10,18 @@ FL = -(H + O)
 BIG = 8192.0
 NONE = W + O + 300
 WW = NONE + 12
-DUM = 1100
+NMAX = (0, 2, 0)
+
+WHO = dict(PC0="v", NF0="v", Q0="v", NE0="v", NE1="v", W1="v", W3="v", W5="v",
+           Q1="a", PC1="a", NF1="a", CC0="a", XZ0="a", XZ1="a", XE00="a", XE01="a", XE02="a", XE03="a", XE10="a", XE11="a",
+           BZ0="a", BZ1="a", W0="a", W2="a", W4="a", W6="a", W7="a")
+G1 = {k: 1 for k in range(8)}
+GL = (G1, G1)
+SHY, TAILW, SLACK = 0.5, 0.001, 0.05
+PR = dict(win=0, off=-3, pc=0, pcB=2, qB=-1, gA=-2, gB=3, cA=3, cB=3, red=-1, mid=-3, mB=-2,
+          xe=2, xB=3, xz0=-2, xz1=-1, prep=3, pB=-3, so0=1, so1=3,
+          pat0=1, pat1=-2, pat2=0, max0=2, max1=-2, max2=-2, dif0=-1, dif1=3, dif2=-3,
+          sum0=0, sum1=3, sum2=3, fin0=-2, fin1=0, fin2=4)
 
 F32, BF, F16, I32, U16 = "float32", "bfloat16", "float16", "int32", "uint16"
 SCRATCH = {}
@@ -21,40 +32,41 @@ def _sb(names, cols, dtype):
         SCRATCH[nm] = ("sbuf", [128] + (cols if isinstance(cols, list) else [cols]), dtype)
 
 
-_sb("SA", [8, 64], I32)
-_sb("SH", [8, 64], F16)
-_sb("L", [8, 4, 16], F16)
-_sb("L2", [4, 8, 16], F16)
+_sb("SA", [8, 4, 16], I32)
+_sb("SH L", [8, 4, 16], F16)
+_sb("L2", [4, 16, 16], F16)
 _sb("WN WI", WW, F32)
 _sb("WX", WW, BF)
 _sb("OFF", 512, U16)
-_sb("S", 8192, F32)
+_sb("S", 8192, F16)
 _sb("EQ", 3072, BF)
-_sb("P16 Q16 RB16 U W16", 512, F16)
+_sb("P16 Q16 PC RB U G BZ", 512, F16)
+_sb("W16", 1024, F16)
 _sb("P32", 768, F32)
-_sb("NF NV TWO GE XZB ED FF", 512, BF)
-_sb("RC32 POS VALS SAT VI", 512, F32)
-_sb("CW", DUM + 516, F32)
-_sb("T1 T2 LI T5 T6", 32, I32)
-_sb("T3 T4 DC", 32, F32)
-_sb("OT OB LP LQ LH", 32, U16)
-_sb("TS", 48, F32)
-_sb("Z1 Z2 Z3 SO1 SO2 DJ OH", 16, F32)
-_sb("E1 QM", 16, BF)
-_sb("SO", 16, U16)
+_sb("NF NV TWO GE XZB ED FF DUP", 512, BF)
+_sb("RC VALS CC", 512, F32)
+_sb("VI", 256, F32)
+_sb("CW", 9 * V, F32)
+_sb("LI", 32, I32)
+_sb("T5 T6 T7", 16, I32)
+_sb("OT OB LO", 32, U16)
+_sb("LP LQ LH LC SO", 16, U16)
+_sb("TS", 32, F32)
+_sb("Z3 SO1 OH SEL SE2", 16, F32)
+_sb("DJ GS", 8, F32)
 _sb("OE", 256, U16)
-_sb("BB ZB E32 G1 NEW", 256, F32)
-_sb("M0 NFE", 256, BF)
+_sb("E32 G1 NEW", 256, F32)
+_sb("M0 NFE ZR ONES T8 MASK", 256, BF)
 _sb("XE MM", 4096, BF)
-_sb("PI", 2, I32)
-_sb("C", 32, F32)
-_sb("QD R0 TMP OQ", 128, BF)
+_sb("PI", 8, I32)
+_sb("C", 48, F32)
+_sb("QD QK R0 OQ MV D2E", 128, BF)
+_sb("DC", 128, F16)
 _sb("I32M R1F", 128, F32)
-_sb("J RP RP16 RPB JZ JZ1 JB JE RK0", 144, BF)
-_sb("CB LM", 2048, BF)
-_sb("REP RG ONES", 1024, BF)
+_sb("J RP RPH RP16 JZ JZ1 JB JE JE2", 144, BF)
+_sb("CB", 2048, BF)
+_sb("REP RG ON8", 1024, BF)
 _sb("M", 32 * 128, BF)
-_sb("SEL ONF", 24, F32)
 for _b in range(8):
     SCRATCH["B%d" % _b] = ("psum", [128, 512], F32)
 SCRATCH["XS"] = ("dram", [8, 128, 64], BF)
@@ -65,10 +77,11 @@ SCRATCH["YR"] = ("dram", [8, 128, 64], F32)
 SEMAPHORES = (["cv", "ca", "ct", "cg", "sent", "ld", "xs", "x0", "x1", "xa", "ys", "yo"]
               + ["sa%d" % i for i in range(N)] + ["ya%d" % i for i in range(N)])
 
-MATS = ["I", "BD", "SHF", "IS", "TA0", "TB0", "TC0", "TA1", "TB1", "TC1", "DM", "PERM", "IB", "NBD", "LO1",
-        "NHI", "N0", "N1", "M10", "M11", "M20", "M21", "ZERO", "BDB", "NBDB", "BD4", "NI", "G1", "G2"]
-COLS = ["p", "pd", "pm", "pd16", "wb", "o1", "bb0", "bb1", "bc0", "bc1", "thr", "ini", "sat", "vb",
-        "lp", "lq", "xo", "dc", "dj", "t1", "t2", "t3", "t4"]
+MATS = ["I", "BD", "SHF", "IS", "TA0", "TA1", "TC", "D2", "K5", "PERM", "IB", "NBD", "LO0", "LO1", "NHI", "N0", "N1",
+        "M10", "M11", "M20", "M21", "ZERO", "BDB", "BD4", "NI", "NO", "G1", "G2", "V1", "V2", "V3"]
+COLS = ["p", "pd", "g4", "hb", "p3", "p03", "pm", "pd16", "h0", "mv", "wb0", "wb1", "o1", "bb0", "bb1", "bc0", "bc1",
+        "thr", "vb", "lp", "lo", "xo", "shf", "up", "dn", "d0", "dm", "dp", "le9", "k5", "ev", "s1", "s2", "w2",
+        "t1", "t2", "t3", "t4", "t5"]
 
 
 def plan(src, cores, topo):
@@ -102,24 +115,25 @@ def rank_program(g, core, T, topo):
     cores = list(T.cores)
     queue = {"v": g.vector, "a": g.scalar, "t": g.tensor, "g": g, "s": g.sync}
     csem = {"v": "cv", "a": "ca", "t": "ct", "g": "cg"}
-    ops, hist, total, flat = [], {}, {}, {}
+    ops, hist, total, flat, last, group, pair, prio = [], {}, {}, {}, {}, {}, [], [0]
 
     def A(name, *idx):
         if name not in SCRATCH:
-            return {"ap": T[name][idx], "reg": []}
-        shape = SCRATCH[name][1]
+            return {"ap": T[name][idx], "reg": [], "n": 0, "dt": None, "ps": False}
+        where, shape, dtype = SCRATCH[name]
         if len(idx) == 0:
             idx = (slice(None),)
-        if SCRATCH[name][0] == "sbuf":
+        n = 0
+        if where != "dram":
             if name not in flat:
                 flat[name] = np.arange(int(np.prod(shape[1:]))).reshape(shape[1:])
             f = flat[name][idx[1:]] if len(idx) > 1 else flat[name]
-            lo, hi = int(np.min(f)), int(np.max(f)) + 1
-        elif SCRATCH[name][0] == "dram" and isinstance(idx[0], int):
+            lo, hi, n = int(np.min(f)), int(np.max(f)) + 1, int(np.size(f))
+        if where == "dram" and isinstance(idx[0], int):
             lo, hi = idx[0], idx[0] + 1
-        else:
+        elif where != "sbuf":
             lo, hi = 0, 1 << 30
-        return {"ap": T[name][idx], "reg": [(name, lo, hi)]}
+        return {"ap": T[name][idx], "reg": [(name, lo, hi)], "n": n, "dt": dtype, "ps": where == "psum"}
 
     al = slice(None)
 
@@ -127,12 +141,25 @@ def rank_program(g, core, T, topo):
         return A(name, al, slice(lo, hi, step) if step != 1 else slice(lo, hi))
 
     def ind(win, off):
-        return {"ap": win["ap"].indirect(off["ap"]), "reg": win["reg"], "off": off["reg"]}
+        return {"ap": win["ap"].indirect(off["ap"]), "reg": win["reg"], "off": off["reg"], "n": 16 * off["n"],
+                "dt": win["dt"], "ps": False}
 
     def val(x):
         return x["ap"] if isinstance(x, dict) else x
 
-    def rec(eng, call, outs, ins, sem=None, inc=16):
+    def either(on_vector, on_scalar, key=None):
+        if key in WHO:
+            return on_scalar() if WHO[key] == "a" else on_vector()
+        pair.append([])
+        on_vector()
+        on_scalar()
+        (cv, outs, ins, tv), (ca, _, more, ta) = pair.pop()
+        rec("?", {"v": cv, "a": ca}, outs, ins + more, {"v": tv, "a": ta})
+
+    def rec(eng, call, outs, ins, cost, sem=None, inc=16, hold=None, acc=None):
+        if pair:
+            pair[-1].append((call, outs, ins, cost))
+            return
         rd, wr = [], []
         for x in ins:
             if isinstance(x, dict):
@@ -141,15 +168,17 @@ def rank_program(g, core, T, topo):
             wr += x["reg"]
             rd += x.get("off", [])
         me = len(ops)
-        deps = set()
+        deps, after = set(), set()
         for regs, isw in ((rd, False), (wr, True)):
             for nm, lo, hi in regs:
                 ps = SCRATCH[nm][0] == "psum"
                 for (l2, h2, o2, w2) in hist.get(nm, []):
                     if l2 < hi and lo < h2:
                         other = ops[o2]
-                        same = other["eng"] == eng and other["sem"] is None and sem is None
+                        same = other["eng"] == eng != "?" and other["sem"] is None and sem is None
                         if same and eng == "t":
+                            if ps and not (other["acc"] is acc and acc["first"] != o2):
+                                after.add(o2)
                             continue
                         if sem is not None and other["sem"] == sem:
                             continue
@@ -158,46 +187,83 @@ def rank_program(g, core, T, topo):
         for regs, isw in ((rd, False), (wr, True)):
             for nm, lo, hi in regs:
                 h = hist.setdefault(nm, [])
-                if isw and sem is None:
+                if isw and sem is None and (acc is None or acc["first"] == me):
                     h[:] = [e for e in h if not (lo <= e[0] and e[1] <= hi)]
                 h.append((lo, hi, me, isw))
         if sem is not None:
             total[sem] = total.get(sem, 0) + inc
-        ops.append({"eng": eng, "call": call, "deps": deps, "sem": sem, "sig": False, "n": 0})
+        if eng != "x" and (eng == "g" or sem is not None):
+            if eng in last:
+                after.add(last[eng])
+            last[eng] = me
+        ops.append({"eng": eng, "call": call, "deps": deps, "after": after, "sem": sem, "sig": False, "n": 0,
+                    "cost": cost, "hold": cost if hold is None else hold, "prio": prio[0], "acc": acc})
+
+    CY = 0.00083
+
+    def cost(out, ins, fix, twice=False):
+        full = [x for x in [out] + ins if isinstance(x, dict) and x["n"] > 1]
+        if "off" in out:
+            return 0.05 + 3.8 * CY * out["n"]
+        if any("off" in x for x in full):
+            return 0.06 + 1.56 * CY * out["n"]
+        m = 0.5 if fix < 0.05 and all(x["dt"] in (BF, F16, U16) for x in full) else 1.0
+        return fix + CY * max(64, out["n"] * m * (2 if twice else 1))
 
     def ts(out, in0, s1, op0, s2=None, op1=None):
         if op1 is None:
-            rec("v", lambda: g.vector.tensor_scalar(val(out), val(in0), val(s1), None, op0), [out], [in0, s1])
+            rec("v", lambda: g.vector.tensor_scalar(val(out), val(in0), val(s1), None, op0), [out], [in0, s1],
+                cost(out, [in0], 0.03))
         else:
-            rec("v", lambda: g.vector.tensor_scalar(val(out), val(in0), val(s1), val(s2), op0, op1), [out], [in0, s1, s2])
+            rec("v", lambda: g.vector.tensor_scalar(val(out), val(in0), val(s1), val(s2), op0, op1), [out], [in0, s1, s2],
+                cost(out, [in0], 0.03))
 
     def tt(out, a, b, op):
-        rec("v", lambda: g.vector.tensor_tensor(val(out), val(a), val(b), op), [out], [a, b])
+        rec("v", lambda: g.vector.tensor_tensor(val(out), val(a), val(b), op), [out], [a, b],
+            cost(out, [a, b], 0.03, not (a["ps"] or b["ps"])))
 
     def cp(out, a):
-        rec("v", lambda: g.vector.tensor_copy(val(out), val(a)), [out], [a])
+        rec("v", lambda: g.vector.tensor_copy(val(out), val(a)), [out], [a], cost(out, [a], 0.03))
 
     def ms(out, c):
-        rec("v", lambda: g.vector.memset(val(out), c), [out], [])
+        rec("v", lambda: g.vector.memset(val(out), c), [out], [], cost(out, [], 0.03))
 
-    def act(out, a, func, bias=0.0, scale=1.0):
-        rec("a", lambda: g.scalar.activation(val(out), val(a), func, bias=val(bias), scale=val(scale)), [out], [a, bias, scale])
+    def scan(out, a, b, op0, op1):
+        rec("v", lambda: g.vector.tensor_tensor_scan(val(out), val(a), val(b), 0.0, op0, op1), [out], [a, b],
+            cost(out, [a, b], 0.03))
 
-    def mm(out, lhsT, rhs, start=True, stop=True):
-        rec("t", lambda: g.tensor.matmul(val(out), val(lhsT), val(rhs), start, stop), [out], [lhsT, rhs])
+    def act(out, a, func, bias=0.0, scale=1.0, acc=None):
+        if acc is None:
+            rec("a", lambda: g.scalar.activation(val(out), val(a), func, bias=val(bias), scale=val(scale)), [out],
+                [a, bias, scale], cost(out, [a], 0.06))
+        else:
+            rec("a", lambda: g.scalar.activation(val(out), val(a), func, bias=val(bias), scale=val(scale),
+                                                 accum_out=val(acc)), [out, acc], [a, bias, scale], cost(out, [a], 0.08))
+
+    def mm(out, lhsT, rhs, start=True):
+        bank = out["reg"][0][0]
+        if start:
+            group[bank] = {"first": len(ops), "left": 0}
+        grp = group[bank]
+        grp["left"] += 1
+
+        def call():
+            grp["left"] -= 1
+            return g.tensor.matmul(val(out), val(lhsT), val(rhs), start, grp["left"] == 0)
+        rec("t", call, [out], [lhsT, rhs], CY / 2 * max(64, out["n"]) * (4 if rhs["dt"] == F32 else 1), acc=grp)
 
     def iota(out, pat, base, cm):
-        fl = SCRATCH[out["reg"][0][0]][2] != I32
-        if fl:
-            rec("g", lambda: g.iota(val(out), pat, base, cm, allow_small_or_imprecise_dtypes=True), [out], [])
+        c = 0.13 + 2 * CY * out["n"]
+        if out["dt"] != I32:
+            rec("g", lambda: g.iota(val(out), pat, base, cm, allow_small_or_imprecise_dtypes=True), [out], [], c)
         else:
-            rec("g", lambda: g.iota(val(out), pat, base, cm), [out], [])
+            rec("g", lambda: g.iota(val(out), pat, base, cm), [out], [], c)
 
     def asel(out, a, pat, op, base, cm, fill=0.0):
-        rec("g", lambda: g.affine_select(val(out), val(a), pat, op, fill, base, cm), [out], [a])
+        rec("g", lambda: g.affine_select(val(out), val(a), pat, op, fill, base, cm), [out], [a], 0.17 + 2 * CY * out["n"])
 
     def dma(eng, out, a, sem):
-        rec(eng, lambda: queue[eng].dma_start(val(out), val(a)).then_inc(T.sem[sem], 16), [out], [a], sem=sem)
+        rec(eng, lambda: queue[eng].dma_start(val(out), val(a)).then_inc(T.sem[sem], 16), [out], [a], 2.0, sem=sem, hold=0.1)
 
     def send(src_of, dst, sem):
         for call in plan(R, cores, topo):
@@ -208,11 +274,11 @@ def rank_program(g, core, T, topo):
                                              remote_sem=T.sem[sem], src=src_of(q)["ap"], dst=dst["ap"]))
                 n += len(engs)
             rec("g", lambda trs=trs: g.remote_dma_fused(trs, local_sem=T.sem["sent"]), [],
-                [src_of(q) for q, _ in call], sem="sent", inc=n)
+                [src_of(q) for q, _ in call], 1.2, sem="sent", inc=n)
 
-    def arrive(q, out, sem):
+    def arrive(q, out, sem, when):
         n = [len(e) for call in plan(q, cores, topo) for d, e in call if d == R][0]
-        rec("x", None, [out], [], sem=sem, inc=n)
+        rec("x", None, [out], [], when, sem=sem, inc=n)
 
     def M(name):
         i = MATS.index(name)
@@ -228,10 +294,18 @@ def rank_program(g, core, T, topo):
     def B(i, lo=0, hi=512, step=1):
         return cs("B%d" % i, lo, hi, step)
 
+    def hf(name, X, n=256):
+        return cs(name, n * X, n * X + n)
+
     EQo, NE, GT, GE_, LT = ALU.is_equal, ALU.not_equal, ALU.is_gt, ALU.is_ge, ALU.is_lt
     ADD, SUB, MUL, MAX, MIN = ALU.add, ALU.subtract, ALU.mult, ALU.max, ALU.min
-    WB = 7
     WN, WX, WI = A("WN"), A("WX"), A("WI")
+
+    def OH(l):
+        return cs("OH", l, l + 1)
+
+    def ln(out, col, w):
+        ts(out, cs("J", 15, 15 + out["n"]), col, EQo, w, MUL)
 
     def sel(out, a, ap, ax, ak, d, op, fill=0.0):
         asel(M(out), M(a), [[ax, 8], [ak, 16]], op, d, ap, fill)
@@ -251,38 +325,28 @@ def rank_program(g, core, T, topo):
     def aff(out, a, scale, bias):
         act(out, a, ACT.Copy, bias=float(bias), scale=float(scale))
 
+    prio[0] = -9
     for q in range(N):
         dma("s" if q % 2 == 0 else "a", A("SA", al, q), A("stars", slice(16 * q, 16 * q + 16), al), "ld")
     dma("s", A("XS"), A("x", al), "xs")
 
     iota(cs("PI", 0, 1), [[0, 1]], 0, 1)
-    iota(A("R0"), [[0, 8], [-8, 16]], 0, 1)
     iota(A("QD"), [[1, 8], [0, 16]], 0, 0)
-    iota(A("QM"), [[1, 16]], 0, 0)
+    iota(A("QK"), [[0, 8], [1, 16]], 0, 0)
     iota(cs("J", 0, 143), [[1, 143]], -15, 0)
+    iota(A("R0"), [[0, 8], [-8, 16]], 0, 1)
     iota(A("LI"), [[16, 32]], 0, 1)
-    iota(A("VI"), [[1, 512]], 0, 0)
-    ms(cs("WN", 0, O), float(H))
-    ms(cs("WN", W + O, WW), float(H))
-    cp(C("p"), cs("PI", 0, 1))
-    ts(cs("PI", 1, 2), cs("PI", 0, 1), 4, ALU.arith_shift_right)
-    ms(cs("WX", 0, O), 0.0)
-    cp(C("pd"), cs("PI", 1, 2))
-    ms(cs("WX", W + O, WW), 0.0)
-    ts(C("pd16"), C("pd"), 16.0, MUL)
-    ts(M("BD"), A("QD"), C("pd"), EQo)
-    tt(C("pm"), C("p"), C("pd16"), SUB)
+    iota(A("VI"), [[1, 256]], 0, 0)
 
     ts(A("SH"), A("SA"), float(-H), ADD)
     send(lambda q: A("SH", al, q), A("L", al, R), "sa%d" % R)
     send(lambda q: A("XS", q), A("XR", R), "xa")
-    for b in range(4):
-        ts(A("L", al, R, b), A("SA", al, R, slice(16 * b, 16 * b + 16)), float(-H), ADD)
+    ts(A("L", al, R), A("SA", al, R), float(-H), ADD)
     others = [q for q, _ in plan(R, cores, topo)[0][4:]]
     others += [q for q in range(N) if q != R and q not in others]
-    for q in others:
-        arrive(q, A("L", al, q), "sa%d" % q)
-        arrive(q, A("XR", q), "xa")
+    for i, q in enumerate(others):
+        arrive(q, A("L", al, q), "sa%d" % q, 9.5 + 0.3 * i)
+        arrive(q, A("XR", q), "xa", 13.0)
 
     for q in range(N):
         src = A("x", slice(16 * R, 16 * R + 16), al) if q == R else A("XR", q)
@@ -290,72 +354,113 @@ def rank_program(g, core, T, topo):
     for x in range(1, 8):
         dma("s", A("WX", slice(16 * x, 16 * x + 16), slice(O, O + W)), A("WX", slice(0, 16), slice(O, O + W)), "x1")
 
-    ms(A("ONES"), 1.0)
-    ts(A("OH"), A("QM"), C("pm"), EQo)
+    prio[0] = 5
+    for i, (sh, m) in enumerate(((4, 7), (5, 3), (2, 1), (3, 15), (0, 3))):
+        ts(cs("PI", i + 1, i + 2), cs("PI", 0, 1), sh, ALU.arith_shift_right, m, ALU.bitwise_and)
+    cp(cs("C", 0, 6), cs("PI", 0, 6))
+    ms(cs("WN", 0, O), float(H))
+    ms(cs("WN", W + O, WW), float(H))
+    ms(cs("WX", 0, O), 0.0)
+    ms(cs("WX", W + O, WW), 0.0)
+    ts(C("pd16"), C("pd"), 16.0, MUL)
+    ts(M("BD"), A("QD"), C("pd"), EQo)
+    tt(C("pm"), C("p"), C("pd16"), SUB)
+    ts(A("OH"), cs("QK", 0, 16), C("pm"), EQo)
     ts(cs("RP", 0, 143), cs("J", 0, 143), C("pd16"), EQo)
     for vh in range(8):
         ts(cs("REP", 128 * vh, 128 * vh + 128), A("R0"), float(vh), EQo)
-    aff(C("wb"), C("pd"), 512, -H)
-    aff(C("lp"), C("pd"), 496, O)
-    aff(C("dc"), C("pd"), -16, DUM)
-    aff(C("dj"), C("pd"), -16, V)
-    aff(C("xo"), C("pd"), -512, -O)
-    aff(C("lq"), C("pd"), 48, O)
-    aff(M("NBD"), M("BD"), -1, 0)
-    aff(M("BDB"), M("BD"), BIG, 0)
-    aff(M("NBDB"), M("BD"), -BIG, 0)
-    aff(C("t1"), C("pm"), 512, O + 16 * FL)
-    aff(C("ini"), C("pm"), 32, 0)
-    aff(C("t2"), C("pm"), 32, 32.5)
-    aff(C("bb0"), C("pm"), -BIG, 0)
-    aff(C("bc0"), C("pm"), -BIG, -BIG - FL)
-    act(B(WB), A("VI"), ACT.Identity, bias=C("wb"))
+    ts(C("mv"), C("p3"), 4.0, MUL, C("p03"), ADD)
+    ln(cs("MV", 0, 64), C("mv"), 1.0)
+    aff(C("h0"), C("hb"), -1, 1)
+    aff(C("lp"), C("pd"), 240, 0)
+    aff(C("lo"), C("pd"), 496, O)
+    for X in range(2):
+        aff(C("wb%d" % X), C("pd"), 256, -H * X)
     for l in range(16):
         l = (l + 1) % 16
-        act(cs("CB", 128 * l, 128 * l + 128), M("BD"), ACT.Identity, scale=cs("OH", l, l + 1))
-    aff(M("BD4"), M("BD"), W, 0)
-    aff(cs("RPB", 0, 143), cs("RP", 0, 143), BIG, 0)
-    asel(M("I"), cs("ONES", 0, 128), [[1, 128]], EQo, 0, -1)
-    iota(A("T5"), [[16, 4], [512, 8]], 0, 1)
-    iota(A("T6"), [[1, 2], [2, 8], [0, 2]], 0, 0)
-    iota(A("TMP"), [[0, 8], [1, 16]], -5, 0)
-    for k in range(5):
-        asel(A("OQ" if k % 2 == 0 else "TMP"), A("TMP" if k % 2 == 0 else "OQ"), [[0, 8], [1, 16]], NE, -k, 0, float(k + 11))
-    ts(A("LP"), A("LI"), C("lp"), ADD)
-    ms(cs("CW", 0, 264), float(NONE))
+        act(cs("CB", 128 * l, 128 * l + 128), M("BD"), ACT.Identity, scale=OH(l))
+    for i in range(4):
+        act(cs("W16", 256 * i, 256 * i + 256), A("VI"), ACT.Identity, bias=C("wb%d" % (i // 2)))
+    ts(A("LP"), cs("LI", 0, 16), C("lp"), ADD)
     ms(M("ZERO"), 0.0)
-    ms(A("ONF"), 1.0)
-    ts(A("W16"), A("VI"), C("wb"), ADD)
-    ts(A("DC"), A("LI"), C("dc"), ADD)
-    ts(A("DJ"), cs("LI", 0, 16), C("dj"), ADD)
-    ts(C("thr"), cs("OH", 15, 16), -1.0e6, MUL, C("t1"), ADD)
-    ts(C("sat"), cs("OH", 15, 16), BIG, MUL, C("t2"), ADD)
-    ts(C("t3"), cs("OH", 0, 1), float(-16 * FL), MUL)
-    ts(C("t4"), C("pm"), 5.0, LT, 16.0, MUL)
-    ts(C("vb"), cs("OH", 2, 3), float(-FL), MUL, C("t3"), ADD)
-    ts(C("o1"), C("t4"), C("pm"), ADD, -5.0, ADD)
+    ln(M("I"), C("p"), 1.0)
+    ts(C("t1"), OH(0), 16.0, MUL, -1.0, ADD)
+    tt(C("shf"), C("t1"), C("p"), ADD)
+    ln(M("SHF"), C("shf"), 1.0)
+    tt(M("IS"), M("SHF"), M("I"), ADD)
+    prio[0] = 6
+    ln(M("IB"), C("p"), BIG)
+    ts(M("V1"), A("QK"), C("pm"), GT, BIG, MUL)
+    tt(M("TC"), M("V1"), M("BD"), MUL)
+    tt(M("TA0"), M("TC"), M("IB"), SUB)
+    aff(C("bb0"), C("pm"), -BIG, 0)
+    aff(C("bc0"), C("pm"), -BIG, -BIG - FL)
+    aff(C("t2"), C("pm"), -V, V + H - 15 * FL + 0.5)
+    aff(C("up"), C("p"), 1, 1)
+    aff(C("dn"), C("p"), 1, -1)
+    aff(C("s2"), C("g4"), 1, 8)
+    aff(C("w2"), OH(1), -1024, 0)
+    aff(C("xo"), C("pd"), -V, H)
+    ts(C("t3"), OH(0), 1.0e6, MUL, C("t2"), ADD)
+    ts(C("t4"), C("pm"), 8.5, GT, -1.0e6, MUL)
+    tt(C("thr"), C("t3"), C("t4"), ADD)
+    ts(C("le9"), C("pm"), 9.5, LT)
+    ts(C("dp"), C("pm"), 8.5, LT, -0.5, MUL)
+    ts(C("dm"), C("le9"), OH(0), SUB, -0.5, MUL)
+    ts(C("d0"), C("dm"), C("dp"), ADD, -1.0, MUL)
+    aff(C("k5"), C("le9"), V, 0)
+    ln(M("V1"), C("p"), C("d0"))
+    ln(M("V2"), C("dn"), C("dm"))
+    ln(M("V3"), C("up"), C("dp"))
+    tt(M("V1"), M("V1"), M("V2"), ADD)
+    tt(M("D2"), M("V1"), M("V3"), ADD)
+    ln(M("K5"), C("p"), C("k5"))
+    ts(C("t5"), C("g4"), 2.0, MUL, 1.0, ADD)
+    tt(C("ev"), C("t5"), C("pd"), SUB)
+    ms(cs("D2E", 0, 16), 0.0)
+    ts(cs("D2E", 16, 128), cs("M", 128 * MATS.index("D2"), 128 * MATS.index("D2") + 112), C("ev"), MUL)
+    ts(C("vb"), OH(0), float(-16 * FL), MUL, -NONE / 2, ADD)
+    ts(C("s1"), C("pm"), 4.0, MUL, C("g4"), ADD)
+    ln(cs("SEL", 0, 12), C("s1"), 1.0)
+    ln(cs("SE2", 0, 12), C("s2"), C("w2"))
+    tt(cs("SEL", 0, 12), cs("SEL", 0, 12), cs("SE2", 0, 12), ADD)
+    ms(A("ZR"), 0.0)
+    ms(A("ONES"), 1.0)
+    aff(cs("RPH", 0, 143), cs("RP", 0, 143), 0.5, 0)
+    aff(cs("RP16", 0, 143), cs("RP", 0, 143), 1.0 / 16, 0)
+    aff(A("R1F"), red("RP", 1), 1, 0)
+    ts(A("LO"), A("LI"), C("lo"), ADD)
+    prio[0] = 7
+    iota(A("T6"), [[1, 2], [2, 4], [0, 2]], 0, 0)
+    iota(A("T5"), [[16, 2], [256, 8]], 0, 1)
+    iota(A("T7"), [[-16, 2], [V, 8]], V + 31, -1)
+    iota(A("T8"), [[-16, 2], [0, 4], [1, 32]], 0, 0)
+
+    def refill():
+        for a in range(1, 9):
+            iota(cs("CW", V * a, V * a + 32), [[0, 32]], NONE // 2, 0)
+
+    refill()
+    iota(WI, [[1, WW]], 0, 0)
+    ts(A("LC"), A("T7"), C("pd16"), ADD)
+    ts(A("MASK"), A("T8"), C("pm"), GT)
+    cp(A("LH"), A("T6"))
+    ts(A("DJ"), cs("LI", 0, 8), C("lo"), ADD, float(V + FL), ADD)
     cp(cs("JZ1", 0, 8), cs("RP", 0, 8))
     tt(cs("JZ1", 8, 143), cs("RP", 8, 143), cs("RP", 0, 135), ADD)
-    ts(A("LQ"), A("T5"), C("lq"), ADD)
-    cp(A("LH"), A("T6"))
-    ts(A("QD"), A("OQ"), C("o1"), GT, BIG, MUL)
-    tt(M("TC1"), A("QD"), M("BD"), MUL)
-    line("G1", "BD", -1)
-    sel("SHF", "G1", 16, -256, -1, 15, NE, 1.0)
-    diag("IS", "SHF", 0, 1.0)
-    sel("TC0", "BDB", -1, 16, 1, 0, GT)
-    diag("TA0", "TC0", 0, -BIG)
-    sel("G1", "NBDB", -1, 16, 1, 0, GT)
-    diag("TB0", "G1", 0, BIG)
-    line("G2", "NBD", -1)
-    sel("G1", "G2", 16, -256, -1, 15, NE, -1.0)
-    diag("G2", "G1", 0, 1.0)
-    sel("DM", "G2", 0, 0, 1, -14, NE)
-    asel(A("SEL"), A("ONF"), [[-1, 3], [-16, 8]], EQo, 0, 1)
-    line("IB", "BDB", 0)
-    sel("LO1", "BD", 0, 0, -1, 8, GT)
+    aff(cs("JB", 0, 143), cs("RP", 0, 143), -2, 0)
+    aff(cs("JE", 0, 143), cs("RP", 0, 143), -1, 0)
+    aff(cs("JZ", 0, 143), cs("JZ1", 0, 143), 2, 0)
+    aff(cs("JE2", 0, 143), cs("JZ1", 0, 143), -1, 0)
+    aff(A("I32M"), M("I"), 1, 0)
+    aff(M("NI"), M("I"), -1, 0)
+    aff(M("NO"), M("I"), BIG + H, 0)
+    aff(M("NBD"), M("BD"), -1, 0)
+    aff(M("BDB"), M("BD"), BIG, 0)
+    aff(M("BD4"), M("BD"), W, 0)
+    sel("LO0", "BD", 0, 0, -1, 8, GT)
+    asel(M("LO1"), M("LO0"), [[0, 64], [-1, 2]], GT, 1, 0)
     sel("NHI", "NBD", 0, 0, 1, -8, GE_)
-    line("NI", "NBD", 0)
     diag("G1", "IB", 8, BIG)
     rows("G2", "G1", 0, None)
     rows("N0", "G2", None, 7)
@@ -373,300 +478,334 @@ def rank_program(g, core, T, topo):
     rows("G1", "G2", 0, None)
     rows("G2", "G1", None, 7, BIG)
     rows("M21", "G2", None, 15)
-    diag("TA1", "TC1", 0, -BIG)
-    for s in range(16):
-        asel(cs("LM", 128 * s, 128 * s + 128), red("RPB", s), [[1, 128]], GT, 0, -1)
-    iota(cs("WI", H, WW), [[1, WW - H]], H, 0)
-    asel(A("RG"), A("ONES"), [[-16, 8], [0, 8], [-1, 16]], EQo, 0, 1)
-    asel(M("PERM"), cs("ONES", 0, 128), [[-1, 16], [-16, 8]], EQo, 0, 1)
+    prio[0] = 8
+    iota(A("ON8"), [[0, 1024]], 1, 0)
+    asel(A("RG"), A("ON8"), [[-16, 8], [0, 8], [-1, 16]], EQo, 0, 1)
+    asel(M("PERM"), cs("ON8", 0, 128), [[-1, 16], [-16, 8]], EQo, 0, 1)
+    ts(A("LQ"), A("T5"), C("pd16"), ADD)
+    ts(M("V2"), A("QK"), 5.0, LT, 16.0, MUL)
+    tt(A("OQ"), M("V2"), A("QK"), ADD)
+    ts(C("t4"), C("pm"), 5.0, LT, 16.0, MUL)
+    tt(C("o1"), C("t4"), C("pm"), ADD)
+    ts(M("V2"), A("OQ"), C("o1"), GT, BIG, MUL)
+    tt(M("TC"), M("V2"), M("BD"), MUL)
+    tt(M("TA1"), M("TC"), M("IB"), SUB)
+    aff(C("bb1"), C("o1"), -BIG, 5 * BIG)
+    aff(C("bc1"), C("o1"), -BIG, 4 * BIG - FL)
+
+    def copy(out, a, key=None):
+        either(lambda: cp(out, a), lambda: act(out, a, ACT.Copy), key)
 
     def wcopy(i, q, bank):
-        dst = cs("WN", O + V * q, O + V * q + V)
-        if i % 2 == 0:
-            act(dst, B(bank), ACT.Copy)
-        else:
-            cp(dst, B(bank))
+        copy(cs("WN", O + V * q, O + V * q + V), B(bank), "W%d" % i)
 
-    for t in range(RO):
+    def sub(X):
+        return cs("WN", O + H * (1 - X), O + H * (2 - X))
+
+    def window(t):
+        prio[0] = PR["win"]
         if t == 0:
-            order = [R] + others
-            for i, q in enumerate(order):
-                bank = (2, 3, 4, 6)[i % 4]
-                cp(A("L2", al, al, q), A("L", al, q))
+            for i, q in enumerate([R] + others):
+                bank = 4 + i % 4
                 for vh in range(8):
                     mm(B(bank, 64 * vh, 64 * vh + 64), cs("REP", 128 * vh, 128 * vh + 128), A("L", al, q))
-                if i == N - 1:
-                    for b in range(4):
-                        mm(B(5, b, 512, 4), A("L2", al, b), M("I"))
-                    ts(A("OFF"), B(5), float(-FL), ADD)
-                wcopy(i + 1, q, bank)
-            cp(A("P16"), ind(WN, A("LP")))
-            ts(A("NF"), A("P16"), float(H), EQo)
+                wcopy(i + 10, q, bank)
+                for h in range(2):
+                    ts(A("L2", al, al, 8 * (1 - q // 4) + 2 * (q % 4) + h), A("L", al, q), C("hb" if h else "h0"), MUL)
+            for X in range(2):
+                prio[0] = PR["off"] if X == 0 else PR["pc"]
+                for b in range(4):
+                    mm(B(3 - 2 * X, b, 256, 4), A("L2", al, b, slice(8 * X, 8 * X + 8)), cs("MV", 0, 64))
+                ts(hf("OFF", X), B(3 - 2 * X, 0, 256), float(-FL), ADD)
         else:
-            ts(A("P16"), cs("P32", 0, V), float(-H), ADD)
-            for q in range(N):
-                bank = (2, 3, 4, 6)[q % 4]
-                mm(B(bank), cs("RG", 128 * q, 128 * q + 128), A("P16"))
-                wcopy(q, q, bank)
-                if q >= 4:
-                    for s in range(4 * q - 16, 4 * q - 12):
-                        mm(B(1, 0, 32), red("RK0", s), cs("P16", s, V, 16), s == 0, s == 15)
-            ts(cs("OFF", 0, 32), B(1, 0, 32), float(-FL), ADD)
-            cp(A("Q16"), ind(WN, A("LQ")))
-            for b in range(4):
-                mm(B(5, b, 512, 4), cs("Q16", 128 * b, 128 * b + 128), M("PERM"))
-
-        def Sk(k):
-            return cs("S", V * k, V * k + V)
-
-        def eqt(k, c):
-            i = 2 * (k % 3) + c
-            return cs("EQ", V * i, V * i + V)
-
-        def cb(k):
-            l = (k + 1) % 16
-            mm(B(2 + k % 3), cs("CB", 128 * l, 128 * l + 128), A("P16"))
-
-        def eqw(k):
-            tt(eqt(k, 0), Sk(k), B(WB), EQo)
-            mm(B(0), red("RP", k), eqt(k, 0), k == 0, k == 15)
-            if k == 8:
-                mm(B(0), M("I"), A("NF"), False, False)
-
-        def eqc(k):
-            tt(eqt(k, 1), Sk(k), B(2 + k % 3), EQo)
-            mm(B(1), red("RP", k), eqt(k, 1), k == 0, k == 15)
-            if k == 8:
-                mm(B(1), M("IS"), A("NF"), False, False)
-            if k + 3 < 16:
-                cb(k + 3)
-
-        def gather(k):
-            act(Sk(k), ind(WN, cs("OFF", 32 * k, 32 * k + 32)), ACT.Copy)
-
-        gather(0)
-        if t > 0:
-            act(A("NF"), cs("P32", 0, V), ACT.Relu, bias=float(1 - W))
-        for k in range(3):
-            cb(k)
-        if t > 0:
-            ts(cs("OFF", 32, 96), B(5, 32, 96), float(-FL), ADD)
-        eqw(0)
-        if t > 0:
-            ts(cs("OFF", 96, V), B(5, 96, V), float(-FL), ADD)
-        for k in range(1, 16):
-            gather(k)
+            for h in range(2):
+                either(lambda: ts(hf("P16", h), hf("P32", h), float(-H), ADD), lambda: aff(hf("P16", h), hf("P32", h), 1, -H))
+            for i, q in enumerate((4, 5, 6, 7, 0, 1, 2, 3)):
+                prio[0] = PR["win"] + 0.05 * i
+                mm(B(4 + i % 4), cs("RG", 128 * q, 128 * q + 128), A("P16"))
+                wcopy(i, q, 4 + i % 4)
+            for X in range(2):
+                prio[0] = PR["off"] if X == 0 else PR["qB"]
+                copy(hf("Q16", X), ind(sub(X), A("LQ")), "Q%d" % X)
+                prio[0] = PR["off"]
+                for b in range(2):
+                    mm(B(3 + 4 * X, b, 256, 2), cs("Q16", 256 * X + 128 * b, 256 * X + 128 * b + 128), M("PERM"))
+                ts(hf("OFF", X), B(3 + 4 * X, 0, 256), float(-FL), ADD)
+        for X in range(2):
+            prio[0] = PR["pcB" if X else "pc"]
+            copy(hf("PC", X), ind(sub(X), A("LP")), "PC%d" % X)
+            either(lambda: ts(hf("NF", X), hf("PC", X), float(H), EQo),
+                   lambda: act(hf("NF", X), hf("PC", X), ACT.Relu, bias=float(1 - H)), "NF%d" % X)
         if t == 0:
-            aff(cs("RP16", 0, 143), cs("RP", 0, 143), 1.0 / 16, 0)
-            aff(A("R1F"), red("RP", 1), 1, 0)
-            act(A("SAT"), A("VI"), ACT.Identity, bias=C("sat"), scale=0.0)
-            act(cs("P32", 0, V), ind(WN, A("LP")), ACT.Copy, bias=float(H))
-        eqc(0)
-        for k in range(1, 13):
-            eqw(k)
-            eqc(k)
-        eqw(13)
-        eqw(14)
-        eqw(15)
-        act(A("NV"), B(0), ACT.Sign)
-        if t == 0:
-            aff(cs("WI", 0, V), A("VI"), 1, 0)
-        hs = [(0, 256), (256, 512)]
-        for h, (lo, hi) in enumerate(hs):
-            mm(B(5 + h, 0, 256), M("I"), cs("P16", lo, hi), True, False)
-        eqc(13)
-        mm(B(3), M("SHF"), A("P16"), True, False)
-        eqc(14)
-        for h, (lo, hi) in enumerate(hs):
-            mm(B(5 + h, 0, 256), M("TA%d" % t), cs("NV", lo, hi), False, False)
-        eqc(15)
+            prio[0] = 4
+            act(cs("P32", 0, V), ind(WN, A("LO")), ACT.Copy, bias=float(H))
 
-        mm(B(3), M("TC%d" % t), A("NV"), False, False)
-        for h, (lo, hi) in enumerate(hs):
-            tt(cs("TWO", lo, hi), B(1, lo, hi), cs("NV", lo, hi), LT)
-            mm(B(5 + h, 0, 256), M("TB%d" % t), cs("TWO", lo, hi), False, True)
-        mm(B(3), M("TB%d" % t), A("TWO"), False, True)
-        act(A("RC32"), B(3), ACT.Relu, bias=C("bc%d" % t))
-        for h, (lo, hi) in enumerate(hs):
-            ts(cs("RB16", lo, hi), B(5 + h, 0, 256), C("bb%d" % t), ADD, float(FL), MAX)
-            mm(B(2 + 2 * h, 0, 256), M("BD"), cs("RB16", lo, hi))
-        mm(B(0), red("RP16", 2), A("W16"), True, False)
-        for h, (lo, hi) in enumerate(hs):
-            ts(cs("GE", lo, hi), B(2 + 2 * h, 0, 256), C("thr"), GE_)
-            mm(B(5 + h, 0, 256), M("DM"), cs("GE", lo, hi))
-            if h == 0:
-                mm(B(0), red("RP", 0), A("RB16"), False, False)
-        mm(B(0), A("R1F"), A("RC32"), False, True)
-        if t == 0:
-            aff(cs("WI", V, 2 * V), A("VI"), 1, V)
-        act(A("VALS"), B(0), ACT.Identity, bias=C("vb"))
-        if t == 0:
-            for i in (2, 3):
-                aff(cs("WI", i * V, i * V + V), A("VI"), 1, i * V)
-            aff(cs("JB", 0, 143), cs("RP", 0, 143), -2, 0)
-            aff(cs("JE", 0, 143), cs("RP", 0, 143), -1, 0)
-            aff(cs("JZ", 0, 143), cs("JZ1", 0, 143), 2, 0)
-            aff(A("I32M"), M("I"), 1, 0)
-            aff(M("TB1"), M("TA1"), -1, 0)
-            act(cs("RK0", 0, 143), cs("RP", 0, 143), ACT.Identity, scale=cs("OH", 0, 1))
-            aff(C("bb1"), C("o1"), -BIG, 0)
-            aff(C("bc1"), C("o1"), -BIG, -BIG - FL)
-        for h, (lo, hi) in enumerate(hs):
-            ini = C("ini") if h == 0 else cs("POS", lo - 1, lo)
-            pos, src, sat = cs("POS", lo, hi), B(5 + h, 0, 256), cs("SAT", lo, hi)
-            rec("v", lambda pos=pos, src=src, sat=sat, ini=ini: g.vector.tensor_tensor_scan(
-                val(pos), val(src), val(sat), val(ini), ADD, MIN), [pos], [src, sat, ini])
-        for h, (lo, hi) in enumerate(hs):
-            tt(cs("U", lo, hi), cs("POS", lo, hi), B(5 + h, 0, 256), MUL)
+    ring = [0, 0]
+
+    def complaints(X):
+        prio[0] = PR["cB" if X else "cA"]
+        cnt = (B(2 + X, 0, 256), B(6 + X, 0, 256))
+        mm(cnt[0], M("I"), hf("NF", X))
+        mm(cnt[1], M("IS"), hf("NF", X))
+
+        def compare(kk, c):
+            s0 = 4096 * X + V * kk
+            if c == 0 and kk in GL[X]:
+                prio[0] = PR["gB" if X else "gA"]
+                n = GL[X][kk]
+                act(cs("S", s0, s0 + V * n), ind(WN, cs("OFF", s0 // 16, s0 // 16 + 32 * n)), ACT.Copy)
+            prio[0] = PR["cB" if X else "cA"]
+            if c == 1:
+                for i in range(2):
+                    l = (2 * kk + i + 1) % 16
+                    mm(B(kk % 2, 256 * i, 256 * i + 256), cs("CB", 128 * l, 128 * l + 128), hf("PC", X))
+            e0 = V * (ring[0] % 6)
+            ring[0] += 1
+            tt(cs("EQ", e0, e0 + V), cs("S", s0, s0 + V), B(kk % 2) if c else hf("W16", X, 512), EQo)
+            prio[0] = PR["red"]
+            for i in range(2):
+                mm(cnt[c], red("RP", 2 * kk + i), cs("EQ", e0 + 256 * i, e0 + 256 * i + 256), False)
+
+        for kk in range(6):
+            compare(kk, 0)
+            compare(kk, 1)
+        for c in range(2):
+            compare(6, c)
+            compare(7, c)
+
+    def middle(t, X):
+        prio[0] = PR["mB" if X else "mid"]
+        U1, U2 = (4, 5) if X == 0 else (0, 1)
+        pc, nv, two, rb, rc, ge = (hf(nm, X) for nm in ("PC", "NV", "TWO", "RB", "RC", "GE"))
+        act(nv, B(2 + X, 0, 256), ACT.Sign)
+        tt(two, B(6 + X, 0, 256), nv, MIN)
+        for bank, m0 in ((U1, "I"), (U2, "SHF")):
+            mm(B(bank, 0, 256), M(m0), pc)
+            mm(B(bank, 0, 256), M("TA%d" % t), two, False)
+        mm(B(U2, 0, 256), M("IB"), nv, False)
+        ts(rb, B(U1, 0, 256), C("bb%d" % t), ADD, float(FL), MAX)
+        act(rc, B(U2, 0, 256), ACT.Relu, bias=C("bc%d" % t))
+        mm(B(U1, 256, 512), M("BD"), rb)
+        gs = cs("GS", X, X + 1)
+        act(ge, B(U1, 256, 512), ACT.Sign, bias=C("thr"), acc=gs)
+        scan(hf("G", X), ge, A("ZR"), ADD, ADD)
+        act(A("DC"), A("D2E"), ACT.Identity, scale=gs)
+        mm(B(2 + X, 0, 256), M("K5"), A("ONES"))
+        mm(B(2 + X, 0, 256), M("D2"), hf("G", X), False)
+        mm(B(2 + X, 0, 256), A("DC"), A("ONES"), False)
+        tt(hf("U", X), B(2 + X, 0, 256), ge, MUL)
         for s in range(16):
-            mm(B(2, 0, 32), red("RP", s), cs("U", s, V, 16), s == 0, s == 15)
-        ts(A("T1"), B(2, 0, 32), 2.0, MUL)
-        ts(A("T2"), A("T1"), 1, ALU.bitwise_and)
-        tt(A("T3"), A("T2"), A("DC"), MUL)
-        tt(A("T4"), B(2, 0, 32), A("T3"), MAX)
-        cp(A("OT"), A("T4"))
-        cp(ind(A("CW"), A("OT")), A("VALS"))
+            mm(B(U1, 0, 16), red("RPH", s), cs("U", 256 * X + s, 256 * X + 256, 16), s == 0)
+        ts(hf("OT", X, 16), B(U1, 0, 16), float(H - 1), ADD)
+        mm(B(U2, 256, 512), red("RP16", 2), cs("W16", 512 * X, 512 * X + 256))
+        mm(B(U2, 256, 512), red("RP", 0), rb, False)
+        mm(B(U2, 256, 512), A("R1F"), rc, False)
+        act(hf("VALS", X), B(U2, 256, 512), ACT.Identity, bias=C("vb"))
+        cp(ind(A("CW"), hf("OT", X, 16)), hf("VALS", X))
+        copy(hf("CC", X), ind(A("CW"), A("LC")), "CC%d" % X)
+        for jh in range(2):
+            mm(B(U2, jh, 24, 2), cs("CC", 256 * X + 128 * jh, 256 * X + 128 * jh + 128), cs("SEL", 0, 12))
+        if (t, X) != (RO - 1, 1):
+            refill()
+        obz, obb = cs("OB", 16 * X, 16 * X + 8), cs("OB", 16 * X + 8, 16 * X + 16)
+        cp(obb, B(U2, 0, 8))
+        ts(hf("OE", X, 128), ind(WN, obb), float(-FL), ADD)
+        ts(hf("TS", X, 16), B(U2, 0, 16), float(FL), ADD)
+        tt(hf("Z3", X, 8), cs("TS", 16 * X + 8, 16 * X + 16), B(U2, 16, 24), MAX)
+        ts(obz, hf("Z3", X, 8), float(-FL), ADD)
+
+    def prepare(X):
+        sb = 6 + X
+        ob, obb = hf("OB", X, 16), cs("OB", 16 * X + 8, 16 * X + 16)
+        prio[0] = PR["xz%d" % X]
+        copy(hf("XZB", X), ind(WX, ob), "XZ%d" % X)
+        prio[0] = PR["xB" if X else "xe"]
+        for i in (2, 3, 0, 1):
+            lo = 2048 * X + 512 * i
+            copy(cs("XE", lo, lo + 512), ind(WX, cs("OE", lo // 16, lo // 16 + 32)), "XE%d%d" % (X, i))
+        prio[0] = PR["pB" if X else "prep"]
+        either(lambda: ts(hf("BZ", X), ind(WI, ob), float(FL), ADD),
+               lambda: act(hf("BZ", X), ind(WI, ob), ACT.Copy, bias=float(FL)), "BZ%d" % X)
+        either(lambda: ts(hf("E32", X, 128), hf("OE", X, 128), float(-O), ADD),
+               lambda: act(hf("E32", X, 128), ind(WN, obb), ACT.Copy, bias=float(H)), "E%d" % X)
+        either(lambda: ts(hf("NFE", X, 128), hf("E32", X, 128), float(W), EQo),
+               lambda: act(hf("NFE", X, 128), hf("E32", X, 128), ACT.Relu, bias=float(1 - W)), "NE%d" % X)
+        mm(B(sb, 0, 128), M("I"), cs("XZB", 256 * X, 256 * X + 128))
+        mm(B(sb, 0, 128), M("NI"), cs("XZB", 256 * X + 128, 256 * X + 256), False)
+        act(hf("M0", X, 128), B(sb, 0, 128), ACT.Abs)
+        prio[0] = PR["so%d" % X]
         for h in range(2):
-            mm(B(1, h, 48, 2), cs("CW", 1 + h, 257 + h, 2), A("SEL"))
+            tt(cs("ED", 256 * X + 128 * h, 256 * X + 128 * h + 128),
+               ind(cs("TS", 16 * X, 16 * X + 8), cs("LH", 8 * h, 8 * h + 8)), cs("BZ", 256 * X + 128, 256 * X + 256), EQo)
+        scan(hf("DUP", X), hf("ED", X), A("MASK"), MAX, MIN)
 
-        OBZ, OBB = cs("OB", 0, 16), cs("OB", 16, 32)
-        pat = {1: 2, 0: 4}
-        acc = {1: 6, 0: 0}
-        cnt = [0]
+    def judge(X, p0, n, nmax, acc, pz, pb, dif, qb):
+        nu = n // 32
+        reps, first = 16 // nu, p0 + n == 128
+        tag = "%d" % (X if first else 2)
+        lo, hi = 2048 * X + 16 * p0, 2048 * X + 16 * (p0 + n)
+        g0 = 128 * X + p0
 
-        def xzb(c, z):
-            return cs("XZB", 256 * z + 128 * c, 256 * z + 128 * c + 128)
-
-        def obs(c, z):
-            return cs("OB", 16 * z + 8 * c, 16 * z + 8 * c + 8)
-
-        def patterns(c):
+        def part(name):
+            return cs(name, g0, g0 + n)
+        xz, xb = (cs("XZB", 256 * X + 128 * z + p0, 256 * X + 128 * z + p0 + n) for z in range(2))
+        prio[0] = PR["pat" + tag]
+        mm(B(acc, 0, 264), M("ZERO"), cs("W16", 0, 264))
+        if first:
+            prio[0] = PR["so%d" % X]
+            mm(B(acc, 256, 264), A("I32M"), cs("TS", 16 * X, 16 * X + 8), False)
+            for h in range(2):
+                e0 = 256 * X + 128 * h
+                mm(B(acc, 256 + h, 264, 2), M("IB"), cs("DUP", e0 + 31, e0 + 128, 32), False)
+        prio[0] = PR["pat" + tag]
+        for bank, x in ((pz, xz), (pb, xb))[:2 if nmax else 1]:
+            for i in range(reps):
+                mm(B(bank, i, 512, reps), M("I"), x)
+        prio[0] = PR["sum" + tag]
+        for ih in range(2):
+            reg = B(acc, n * ih, n * ih + n)
+            mm(reg, M("NBD"), xz, False)
+            if nmax:
+                mm(reg, M("LO%d" % (0 if nmax == nu else 1)), xb, False)
+            mm(reg, M("NHI"), part("M0"), False)
+            mm(reg, M("N%d" % ih), part("NFE"), False)
+        for q in range(nu):
+            bymax = q < nmax
+            xe = cs("XE", lo + q, hi, nu)
+            ks = [q + nu * j for j in range(reps)]
+            regs = [B(acc, n * (k // 8), n * (k // 8) + n) for k in ks]
+            for j, k in enumerate(ks):
+                mm(regs[j], red("JE", 8 + k % 8) if bymax else red("JE2", k % 8), cs("XE", lo + k, hi, 16), False)
             for z in range(2):
-                for i in range(4):
-                    mm(B(pat[c] + z, i, 512, 4), M("I"), xzb(c, z))
-
-        def unit(c, q):
-            lo, hi = 2048 * c, 2048 * c + 2048
-            regs = [B(acc[c], 128 * (j // 2), 128 * (j // 2) + 128) for j in range(4)]
-            for j in range(4):
-                mm(regs[j], red("JE", 8 + (q + 4 * j) % 8), cs("XE", lo + q + 4 * j, hi, 16), False, False)
-            for z in range(2):
-                m0 = V * (cnt[0] % 8)
-                cnt[0] += 1
-                tt(cs("MM", m0, m0 + V), cs("XE", lo + q, hi, 4), B(pat[c] + z), MAX)
-                for j in range(4):
-                    mm(regs[j], red("JB" if z else "JZ", (q + 4 * j) % 8), cs("MM", m0 + j, m0 + V, 4), False,
-                       q == 3 and z == 1 and j == 3)
-
-        def terms(c):
-            for ih in range(2):
-                reg = B(acc[c], 128 * ih, 128 * ih + 128)
-                mm(reg, M("NBD"), xzb(c, 0), False, False)
-                mm(reg, M("LO1"), xzb(c, 1), False, False)
-                mm(reg, M("NHI"), cs("M0", 128 * c, 128 * c + 128), False, False)
-                mm(reg, M("N%d" % ih), cs("NFE", 128 * c, 128 * c + 128), False, False)
-
-        def early(c, qb):
-            lo = 128 * c
-            mm(B(qb, 0, 128), A("I32M"), cs("ZB", lo, lo + 128), True, False)
-            mm(B(qb, 0, 128), M("TA0"), cs("NFE", lo, lo + 128), False, False)
-
-        def flags(c, qb):
-            lo = 128 * c
-            ts(cs("FF", 2 * lo, 2 * lo + 256), B(acc[c], 0, 256), 0.0, LT)
-            for ih in range(2):
-                mm(B(qb, 0, 128), M("M2%d" % ih), cs("FF", 2 * lo + 128 * ih, 2 * lo + 128 * ih + 128), False, ih == 1)
-            for ih in range(2):
-                mm(B(qb, 128, 256), M("M1%d" % ih), cs("FF", 2 * lo + 128 * ih, 2 * lo + 128 * ih + 128), ih == 0, ih == 1)
-
-        def new(c, qb):
-            lo = 128 * c
-            tt(cs("G1", lo, lo + 128), cs("E32", lo, lo + 128), B(qb, 128, 256), MAX)
-            tt(cs("NEW", lo, lo + 128), cs("G1", lo, lo + 128), B(qb, 0, 128), MIN)
-
-        def write(q):
+                m0 = V * (ring[1] % 8)
+                ring[1] += 1
+                prio[0] = PR["max" + tag]
+                if z == 0 or bymax:
+                    tt(cs("MM", m0, m0 + V), xe, B(pb if z else pz), MAX)
+                else:
+                    prio[0] = PR["dif" + tag]
+                    d = dif[q % len(dif)]
+                    mm(B(d), M("I"), xe)
+                    for i in range(reps):
+                        mm(B(d, i, 512, reps), M("NI"), xb, False)
+                    act(cs("MM", m0, m0 + V), B(d), ACT.Abs)
+                prio[0] = PR["sum" + tag]
+                for j, k in enumerate(ks):
+                    mm(regs[j], red("JZ" if z == 0 else "JB" if bymax else "JE", k % 8), cs("MM", m0 + j, m0 + V, reps), False)
+        o1, o2 = B(qb, 0, n), B(qb, n, 2 * n)
+        prio[0] = PR["fin" + tag]
+        mm(o1, M("I"), cs("BZ", 256 * X + p0, 256 * X + p0 + n))
+        mm(o1, M("NO"), cs("ONES", 0, n), False)
+        mm(o1, M("TA0"), part("NFE"), False)
+        ts(cs("FF", 2 * g0, 2 * g0 + 2 * n), B(acc, 0, 2 * n), 0.0, LT)
+        if first:
+            tt(hf("SO1", X, 8), B(acc, 256, 264), A("DJ"), MIN)
+            ts(hf("SO", X, 8), hf("SO1", X, 8), C("xo"), ADD)
+        for ih in range(2):
+            mm(o1, M("M2%d" % ih), cs("FF", 2 * g0 + n * ih, 2 * g0 + n * ih + n), False)
+        for ih in range(2):
+            mm(o2, M("M1%d" % ih), cs("FF", 2 * g0 + n * ih, 2 * g0 + n * ih + n), ih == 0)
+        tt(part("G1"), part("E32"), o2, MAX)
+        tt(part("NEW"), part("G1"), o1, MIN)
+        for q in reversed(range(g0 // 32, (g0 + n) // 32)):
             cp(ind(A("P32"), cs("SO", 2 * q, 2 * q + 2)), cs("NEW", 32 * q, 32 * q + 32))
 
-        cp(OBB, B(1, 0, 16))
-        ts(A("OE"), ind(WN, OBB), float(-FL), ADD)
-        act(A("BB"), ind(WI, OBB), ACT.Copy)
-        act(cs("XE", 2048, 3840), ind(WX, cs("OE", 128, 240)), ACT.Copy)
-        cp(A("TS"), B(1, 0, 48))
-        BW = cs("TS", 0, 16)
-        ts(A("Z1"), cs("TS", 16, 32), 0.0, EQo)
-        tt(cs("E1", 0, 8), cs("TS", 0, 16, 2), cs("TS", 1, 16, 2), EQo)
-        tt(A("Z2"), A("Z1"), cs("TS", 32, 48), MUL)
-        tt(A("Z3"), A("Z2"), cs("TS", 16, 32), ADD)
-        cp(OBZ, A("Z3"))
-        for z in range(2):
-            cp(xzb(1, z), ind(WX, obs(1, z)))
-        patterns(1)
-        for z in range(2):
-            act(xzb(0, z), ind(WX, obs(0, z)), ACT.Copy)
-        act(cs("XE", 0, 2048), ind(WX, cs("OE", 0, 128)), ACT.Copy)
-        cp(cs("XE", 3840, 4096), ind(WX, cs("OE", 240, 256)))
-        for h in range(2):
-            tt(cs("ED", 256 * h, 256 * h + 256), ind(BW, cs("LH", 16 * h, 16 * h + 16)), A("BB"), EQo)
-        mm(B(acc[1], 0, 256), M("ZERO"), cs("NF", 0, 256), True, False)
-        mm(B(1, 0, 32), M("ZERO"), cs("NF", 0, 32), True, False)
-        mm(B(1, 0, 16), A("I32M"), BW, False, False)
-        mm(B(1, 1, 16, 2), M("IB"), cs("E1", 0, 8), False, False)
-        for s in range(16):
-            mm(B(1, 0, 32), cs("LM", 128 * s, 128 * s + 128), cs("ED", s, V, 16), False, s == 15)
-        act(A("E32"), ind(WN, OBB), ACT.Copy, bias=float(H))
-        act(A("NFE"), A("E32"), ACT.Relu, bias=float(1 - W))
-        unit(1, 0)
-        ts(A("SO1"), B(1, 0, 16), C("xo"), ADD)
-        tt(A("SO2"), B(1, 16, 32), A("SO1"), ADD)
-        patterns(0)
-        unit(1, 1)
-        tt(A("SO1"), A("SO2"), A("DJ"), MIN)
-        mm(B(1, 0, 256), M("I"), cs("XZB", 0, 256), True, False)
-        mm(B(1, 0, 256), M("NI"), cs("XZB", 256, 512), False, True)
-        act(A("M0"), B(1, 0, 256), ACT.Abs)
-        act(A("ZB"), ind(WI, OBZ), ACT.Copy, bias=BIG - O)
-        if t == 0:
-            aff(cs("CW", 0, 264), cs("VI", 0, 264), 0, NONE)
-        unit(1, 2)
-        cp(A("SO"), A("SO1"))
-        mm(B(acc[0], 0, 256), M("ZERO"), cs("NF", 0, 256), True, False)
-        terms(1)
-        unit(1, 3)
-        early(1, 1)
-        unit(0, 0)
-        terms(0)
-        unit(0, 1)
-        flags(1, 1)
-        early(0, 2)
-        unit(0, 2)
-        new(1, 1)
-        unit(0, 3)
-        write(7)
-        write(6)
-        flags(0, 2)
-        write(5)
-        write(4)
-        new(0, 2)
-        for q in (3, 2, 1, 0):
-            write(q)
+    for t in range(RO):
+        window(t)
+        complaints(0)
+        middle(t, 0)
+        prepare(0)
+        complaints(1)
+        middle(t, 1)
+        judge(0, 0, 128, NMAX[0], 2, 4, 5, (5, 6) if NMAX[0] == 0 else (6,), 6)
+        prepare(1)
+        judge(1, 64, 64, NMAX[1], 3, 0, 1, (1, 7) if NMAX[1] == 0 else (7,), 7)
+        judge(1, 0, 64, NMAX[2], 2, 4, 5, (5, 6) if NMAX[2] == 0 else (6,), 6)
 
+    prio[0] = 0
     dma("s", A("YS"), cs("P32", 0, V), "ys")
     dma("a", A("y", slice(16 * R, 16 * R + 16), al), A("P32", slice(16 * R, 16 * R + 16), slice(0, V)), "yo")
     send(lambda q: A("YS", q), A("YR", R), "ya%d" % R)
     for i, q in enumerate(others):
-        arrive(q, A("YR", q), "ya%d" % q)
+        arrive(q, A("YR", q), "ya%d" % q, 1000.0)
         dma("s" if i % 2 == 0 else "a", A("y", slice(16 * q, 16 * q + 16), al), A("YR", q), "yo")
 
+    bysem = {}
+    for i, o in enumerate(ops):
+        if o["sem"] is not None:
+            bysem.setdefault(o["sem"], []).append(i)
+    users = [[] for _ in ops]
+    for i, o in enumerate(ops):
+        o["pre"] = set(o["after"])
+        for d in o["deps"]:
+            o["pre"].update(bysem[ops[d]["sem"]] if ops[d]["sem"] is not None else [d])
+        o["left"], o["ready"] = len(o["pre"]), 0.0
+        for d in o["pre"]:
+            users[d].append(i)
+    for i in reversed(range(len(ops))):
+        o = ops[i]
+        c = min(o["cost"].values()) if o["eng"] == "?" else min(o["cost"], 20.0)
+        o["tail"] = c + max([0.0] + [ops[u]["tail"] + 0.1 for u in users[i]])
+    free = {e: 0.0 for e in list(queue) + ["x"]}
+    ready = {e: [] for e in free}
+
+    def offer(i):
+        for e in ("va" if ops[i]["eng"] == "?" else ops[i]["eng"]):
+            ready[e].append(i)
+
+    def rank(j, e):
+        o = ops[j]
+        return (o["prio"] + (SHY if o["eng"] == "?" and e == "v" else 0) - TAILW * o["tail"], j)
+
+    for i, o in enumerate(ops):
+        if o["left"] == 0:
+            offer(i)
+    order = []
+    while len(order) < len(ops):
+        best = None
+        for e in ("x", "s", "g", "t", "a", "v"):
+            if ready[e]:
+                now = max(free[e], min(ops[i]["ready"] for i in ready[e]))
+                i = min((j for j in ready[e] if ops[j]["ready"] <= now + SLACK), key=lambda j: rank(j, e))
+                start = max(free[e], ops[i]["ready"])
+                if best is None or start < best[0]:
+                    best = (start, i, e)
+        start, i, e = best
+        o = ops[i]
+        if o["eng"] == "?":
+            ready["a" if e == "v" else "v"].remove(i)
+            o["eng"], o["call"], o["cost"], o["hold"] = e, o["call"][e], o["cost"][e], o["cost"][e]
+        ready[e].remove(i)
+        o["pos"] = len(order)
+        order.append(i)
+        if e != "x":
+            free[e] = start + o["hold"]
+        for u in users[i]:
+            p = ops[u]
+            gap = 0.0 if i in p["after"] and i not in p["deps"] else o["cost"] + 0.1
+            p["ready"] = max(p["ready"], start + gap)
+            p["left"] -= 1
+            if p["left"] == 0:
+                offer(u)
+
     for o in ops:
+        latest = {}
+        for d in o["deps"]:
+            e = ops[d]["eng"]
+            if ops[d]["sem"] is None and (e not in latest or ops[d]["pos"] > ops[latest[e]]["pos"]):
+                latest[e] = d
+        o["deps"] = [d for d in o["deps"] if ops[d]["sem"] is not None] + list(latest.values())
         for d in o["deps"]:
             ops[d]["sig"] = True
     done = {}
-    for o in ops:
+    for i in order:
+        o = ops[i]
         if o["sem"] is None and o["sig"]:
             done[o["eng"]] = done.get(o["eng"], 0) + 1
             o["n"] = done[o["eng"]]
     seen = {}
-    for o in ops:
+    for i in order:
+        o = ops[i]
         if o["eng"] == "x":
             continue
         need = {}

@@ -10,18 +10,21 @@ FL = -(H + O)
 BIG = 8192.0
 NONE = W + O + 300
 WW = NONE + 12
-NMAX = (0, 2, 0)
+NMAX = (2, 0, 2, 0)
+ARR = (9.5, 10.5, 10.55, 10.6, 10.65, 11.4, 11.45)
+FIRST = (("Q0", "W5"), ("O0", "Q1"), ("g0", "N1"))
+FIRST0 = (("g0", "N1"),)
 
-WHO = dict(PC0="v", NF0="v", Q0="v", NE0="v", NE1="v", W1="v", W3="v", W5="v",
-           Q1="a", PC1="a", NF1="a", CC0="a", XZ0="a", XZ1="a", XE00="a", XE01="a", XE02="a", XE03="a", XE10="a", XE11="a",
-           BZ0="a", BZ1="a", W0="a", W2="a", W4="a", W6="a", W7="a")
+WHO = dict(Q1="v", W1="v", W3="v", W7="v", XZ1="v", XE13="v", W10="v", W11="v", W16="v",
+           NF1="a", CC1="a", XZ0="a", XE01="a", XE02="a", XE03="a", XE10="a", XE11="a", E0="a",
+           BZ1="a", W0="a", W2="a", W4="a", W6="a", W17="a", NE0="a", NE1="a")
 G1 = {k: 1 for k in range(8)}
 GL = (G1, G1)
 SHY, TAILW, SLACK = 0.5, 0.001, 0.05
-PR = dict(win=0, off=-3, pc=0, pcB=2, qB=-1, gA=-2, gB=3, cA=3, cB=3, red=-1, mid=-3, mB=-2,
-          xe=2, xB=3, xz0=-2, xz1=-1, prep=3, pB=-3, so0=1, so1=3,
-          pat0=1, pat1=-2, pat2=0, max0=2, max1=-2, max2=-2, dif0=-1, dif1=3, dif2=-3,
-          sum0=0, sum1=3, sum2=3, fin0=-2, fin1=0, fin2=4)
+PR = dict(l2=1, win=1, off=-3, pc=4.5, pcB=-3, qB=-2, gA=-3, gB=4.5, cA=-4, cB=-1, red=-3, mid=-4, mB=-3,
+          xe=2, xB=-2, xz0=1, xz1=-2, prep=2, pB=-3, so0=-2, so1=0,
+          pat0=0, pat1=-1, pat2=-4, max0=4, max1=-3, max2=4, dif0=-3, dif1=-3, dif2=-3,
+          je0=0, je1=-1, je2=-3, sum0=-3, sum1=-4, sum2=4.5, fin0=-1, fin1=4.5, fin2=4.5)
 
 F32, BF, F16, I32, U16 = "float32", "bfloat16", "float16", "int32", "uint16"
 SCRATCH = {}
@@ -34,7 +37,7 @@ def _sb(names, cols, dtype):
 
 _sb("SA", [8, 4, 16], I32)
 _sb("SH L", [8, 4, 16], F16)
-_sb("L2", [4, 16, 16], F16)
+_sb("L2", [2, 4, 4, 16], F16)
 _sb("WN WI", WW, F32)
 _sb("WX", WW, BF)
 _sb("OFF", 512, U16)
@@ -60,13 +63,13 @@ _sb("M0 NFE ZR ONES T8 MASK", 256, BF)
 _sb("XE MM", 4096, BF)
 _sb("PI", 8, I32)
 _sb("C", 48, F32)
-_sb("QD QK R0 OQ MV D2E", 128, BF)
+_sb("QD QK R0 OQ D2E", 128, BF)
 _sb("DC", 128, F16)
 _sb("I32M R1F", 128, F32)
 _sb("J RP RPH RP16 JZ JZ1 JB JE JE2", 144, BF)
 _sb("CB", 2048, BF)
 _sb("REP RG ON8", 1024, BF)
-_sb("M", 32 * 128, BF)
+_sb("M", 36 * 128, BF)
 for _b in range(8):
     SCRATCH["B%d" % _b] = ("psum", [128, 512], F32)
 SCRATCH["XS"] = ("dram", [8, 128, 64], BF)
@@ -74,13 +77,13 @@ SCRATCH["XR"] = ("dram", [8, 128, 64], BF)
 SCRATCH["YS"] = ("dram", [8, 128, 64], F32)
 SCRATCH["YR"] = ("dram", [8, 128, 64], F32)
 
-SEMAPHORES = (["cv", "ca", "ct", "cg", "sent", "ld", "xs", "x0", "x1", "xa", "ys", "yo"]
+SEMAPHORES = (["cv", "ca", "ct", "cg", "sent", "ld", "xs", "x0", "x1", "xa", "ys", "yo", "pc0", "pc1", "pd0", "pd1", "p16"]
               + ["sa%d" % i for i in range(N)] + ["ya%d" % i for i in range(N)])
 
-MATS = ["I", "BD", "SHF", "IS", "TA0", "TA1", "TC", "D2", "K5", "PERM", "IB", "NBD", "LO0", "LO1", "NHI", "N0", "N1",
-        "M10", "M11", "M20", "M21", "ZERO", "BDB", "BD4", "NI", "NO", "G1", "G2", "V1", "V2", "V3"]
-COLS = ["p", "pd", "g4", "hb", "p3", "p03", "pm", "pd16", "h0", "mv", "wb0", "wb1", "o1", "bb0", "bb1", "bc0", "bc1",
-        "thr", "vb", "lp", "lo", "xo", "shf", "up", "dn", "d0", "dm", "dp", "le9", "k5", "ev", "s1", "s2", "w2",
+MATS = ["I", "BD", "SHF", "IS", "TA0", "TA1", "TAh0", "TAh1", "I64", "TC", "D2", "K5", "PERM", "IB", "NBD", "LO0", "LO1",
+        "NHI", "N0", "N1", "M10", "M11", "M20", "M21", "BDB", "BD4", "NI", "NO", "G1", "G2", "V1", "V2", "V3"]
+COLS = ["p", "pd", "g4", "hb", "pm", "pd16", "wb0", "wb1", "o1", "bb0", "bb1", "bc0", "bc1", "bbh0", "bbh1", "bch0", "bch1",
+        "n64", "thr", "vb", "lp", "lo", "xo", "shf", "up", "dn", "d0", "dm", "dp", "le9", "k5", "ev", "s1", "s2", "w2",
         "t1", "t2", "t3", "t4", "t5"]
 
 
@@ -90,10 +93,10 @@ def plan(src, cores, topo):
     near = [q for q in others if topo.chip(cores[q]) == topo.chip(me)]
     far = [q for q in others if q not in near]
 
-    def hops(q):
+    def way(q):
         a, b = topo.chip(me), topo.chip(cores[q])
-        return 1 if (topo.mates(a, b) or topo.same_plane(a, b)) else 2
-    far.sort(key=lambda q: -hops(q))
+        return (topo.mates(a, b) or topo.same_plane(a, b), topo.die(cores[q]) == topo.die(me))
+    far.sort(key=way)
     out = topo.engines(me, cores[far[0]])
     first, second = far[:4], far[4:]
     calls = [[], []]
@@ -265,8 +268,11 @@ def rank_program(g, core, T, topo):
     def dma(eng, out, a, sem):
         rec(eng, lambda: queue[eng].dma_start(val(out), val(a)).then_inc(T.sem[sem], 16), [out], [a], 2.0, sem=sem, hold=0.1)
 
-    def send(src_of, dst, sem):
+    def send(src_of, dst, sem, keep=lambda q: True, engines=None):
         for call in plan(R, cores, topo):
+            call = [(q, engines or e) for q, e in call if keep(q)]
+            if not call:
+                continue
             trs, n = [], 0
             for q, engs in call:
                 rid, pid = topo.addr(cores[q])[:2]
@@ -276,8 +282,8 @@ def rank_program(g, core, T, topo):
             rec("g", lambda trs=trs: g.remote_dma_fused(trs, local_sem=T.sem["sent"]), [],
                 [src_of(q) for q, _ in call], 1.2, sem="sent", inc=n)
 
-    def arrive(q, out, sem, when):
-        n = [len(e) for call in plan(q, cores, topo) for d, e in call if d == R][0]
+    def arrive(q, out, sem, when, n=None):
+        n = n or [len(e) for call in plan(q, cores, topo) for d, e in call if d == R][0]
         rec("x", None, [out], [], when, sem=sem, inc=n)
 
     def M(name):
@@ -326,27 +332,42 @@ def rank_program(g, core, T, topo):
         act(out, a, ACT.Copy, bias=float(bias), scale=float(scale))
 
     prio[0] = -9
+    dma("a", A("XS"), A("x", al), "xs")
     for q in range(N):
-        dma("s" if q % 2 == 0 else "a", A("SA", al, q), A("stars", slice(16 * q, 16 * q + 16), al), "ld")
-    dma("s", A("XS"), A("x", al), "xs")
+        for h in range(2):
+            dma("sa"[h], A("SA", slice(64 * h, 64 * h + 64), q),
+                A("stars", slice(16 * q, 16 * q + 16), slice(256 * h, 256 * h + 256)), "ld")
 
     iota(cs("PI", 0, 1), [[0, 1]], 0, 1)
     iota(A("QD"), [[1, 8], [0, 16]], 0, 0)
     iota(A("QK"), [[0, 8], [1, 16]], 0, 0)
     iota(cs("J", 0, 143), [[1, 143]], -15, 0)
-    iota(A("R0"), [[0, 8], [-8, 16]], 0, 1)
     iota(A("LI"), [[16, 32]], 0, 1)
     iota(A("VI"), [[1, 256]], 0, 0)
 
     ts(A("SH"), A("SA"), float(-H), ADD)
+    near = [q for q in range(N) if topo.chip(cores[q]) == topo.chip(core)]
+    send(lambda q: A("XS", q), A("XR", R), "xa", lambda q: q in near)
     send(lambda q: A("SH", al, q), A("L", al, R), "sa%d" % R)
-    send(lambda q: A("XS", q), A("XR", R), "xa")
+    send(lambda q: A("XS", q), A("XR", R), "xa", lambda q: q not in near)
+    iota(A("T8"), [[-16, 2], [0, 4], [1, 32]], 0, 0)
+    iota(A("T6"), [[1, 2], [2, 4], [0, 2]], 0, 0)
+    iota(A("T5"), [[16, 2], [256, 2], [V, 4]], 0, 1)
+    iota(A("T7"), [[-16, 2], [V, 8]], V + 31, -1)
     ts(A("L", al, R), A("SA", al, R), float(-H), ADD)
-    others = [q for q, _ in plan(R, cores, topo)[0][4:]]
-    others += [q for q in range(N) if q != R and q not in others]
+    others = sorted((q for q in range(N) if q != R),
+                    key=lambda q: (q not in near, R in [d for d, _ in plan(q, cores, topo)[1]]))
     for i, q in enumerate(others):
-        arrive(q, A("L", al, q), "sa%d" % q, 9.5 + 0.3 * i)
+        arrive(q, A("L", al, q), "sa%d" % q, ARR[i])
         arrive(q, A("XR", q), "xa", 13.0)
+
+    for q in sorted([R] + others, key=lambda q: q < 4):
+        for h in range(2):
+            p0, X = 64 * h + 16 * (q % 4), 1 - q // 4
+            dma("s", A("PC", slice(p0, p0 + 16), slice(256 * X, 256 * X + 256)), A("L", slice(64 * h, 64 * h + 64), q), "pc%d" % X)
+    for q in range(N):
+        for h in range(2):
+            dma("s", A("P16", slice(16 * q, 16 * q + 16), slice(256 * h, 256 * h + 256)), A("L", slice(64 * h, 64 * h + 64), q), "p16")
 
     for q in range(N):
         src = A("x", slice(16 * R, 16 * R + 16), al) if q == R else A("XR", q)
@@ -355,9 +376,9 @@ def rank_program(g, core, T, topo):
         dma("s", A("WX", slice(16 * x, 16 * x + 16), slice(O, O + W)), A("WX", slice(0, 16), slice(O, O + W)), "x1")
 
     prio[0] = 5
-    for i, (sh, m) in enumerate(((4, 7), (5, 3), (2, 1), (3, 15), (0, 3))):
+    for i, (sh, m) in enumerate(((4, 7), (4, 3), (6, 1))):
         ts(cs("PI", i + 1, i + 2), cs("PI", 0, 1), sh, ALU.arith_shift_right, m, ALU.bitwise_and)
-    cp(cs("C", 0, 6), cs("PI", 0, 6))
+    cp(cs("C", 0, 4), cs("PI", 0, 4))
     ms(cs("WN", 0, O), float(H))
     ms(cs("WN", W + O, WW), float(H))
     ms(cs("WX", 0, O), 0.0)
@@ -367,25 +388,22 @@ def rank_program(g, core, T, topo):
     tt(C("pm"), C("p"), C("pd16"), SUB)
     ts(A("OH"), cs("QK", 0, 16), C("pm"), EQo)
     ts(cs("RP", 0, 143), cs("J", 0, 143), C("pd16"), EQo)
+    ts(A("R0"), A("QK"), -4.0, MUL, C("p"), ADD)
     for vh in range(8):
-        ts(cs("REP", 128 * vh, 128 * vh + 128), A("R0"), float(vh), EQo)
-    ts(C("mv"), C("p3"), 4.0, MUL, C("p03"), ADD)
-    ln(cs("MV", 0, 64), C("mv"), 1.0)
-    aff(C("h0"), C("hb"), -1, 1)
-    aff(C("lp"), C("pd"), 240, 0)
+        ts(cs("REP", 128 * vh, 128 * vh + 128), A("R0"), float(64 * (vh // 4) + vh % 4), EQo)
+    ts(C("t1"), C("g4"), 2.0, MUL, C("hb"), ADD)
+    aff(C("ev"), C("hb"), -1, 1)
     aff(C("lo"), C("pd"), 496, O)
     for X in range(2):
-        aff(C("wb%d" % X), C("pd"), 256, -H * X)
+        aff(C("wb%d" % X), C("t1"), 256, -H * X)
     for l in range(16):
         l = (l + 1) % 16
         act(cs("CB", 128 * l, 128 * l + 128), M("BD"), ACT.Identity, scale=OH(l))
     for i in range(4):
         act(cs("W16", 256 * i, 256 * i + 256), A("VI"), ACT.Identity, bias=C("wb%d" % (i // 2)))
-    ts(A("LP"), cs("LI", 0, 16), C("lp"), ADD)
-    ms(M("ZERO"), 0.0)
     ln(M("I"), C("p"), 1.0)
-    ts(C("t1"), OH(0), 16.0, MUL, -1.0, ADD)
-    tt(C("shf"), C("t1"), C("p"), ADD)
+    ts(C("t5"), OH(0), 16.0, MUL, -1.0, ADD)
+    tt(C("shf"), C("t5"), C("p"), ADD)
     ln(M("SHF"), C("shf"), 1.0)
     tt(M("IS"), M("SHF"), M("I"), ADD)
     prio[0] = 6
@@ -395,6 +413,13 @@ def rank_program(g, core, T, topo):
     tt(M("TA0"), M("TC"), M("IB"), SUB)
     aff(C("bb0"), C("pm"), -BIG, 0)
     aff(C("bc0"), C("pm"), -BIG, -BIG - FL)
+    TW = "a" in (WHO.get("TW0"), WHO.get("TW1"))
+    if TW:
+        aff(C("bbh0"), C("pm"), -BIG / 2, -BIG / 2)
+        aff(C("bch0"), C("pm"), -BIG / 2, -1.5 * BIG - FL)
+        aff(M("TAh0"), M("TA0"), 0.5, 0)
+        aff(M("I64"), M("I"), 64, 0)
+        ms(C("n64"), -64.5)
     aff(C("t2"), C("pm"), -V, V + H - 15 * FL + 0.5)
     aff(C("up"), C("p"), 1, 1)
     aff(C("dn"), C("p"), 1, -1)
@@ -415,10 +440,8 @@ def rank_program(g, core, T, topo):
     tt(M("V1"), M("V1"), M("V2"), ADD)
     tt(M("D2"), M("V1"), M("V3"), ADD)
     ln(M("K5"), C("p"), C("k5"))
-    ts(C("t5"), C("g4"), 2.0, MUL, 1.0, ADD)
-    tt(C("ev"), C("t5"), C("pd"), SUB)
-    ms(cs("D2E", 0, 16), 0.0)
-    ts(cs("D2E", 16, 128), cs("M", 128 * MATS.index("D2"), 128 * MATS.index("D2") + 112), C("ev"), MUL)
+    ms(cs("D2E", 0, 64), 0.0)
+    ts(cs("D2E", 64, 128), cs("M", 128 * MATS.index("D2"), 128 * MATS.index("D2") + 64), C("ev"), MUL)
     ts(C("vb"), OH(0), float(-16 * FL), MUL, -NONE / 2, ADD)
     ts(C("s1"), C("pm"), 4.0, MUL, C("g4"), ADD)
     ln(cs("SEL", 0, 12), C("s1"), 1.0)
@@ -429,12 +452,7 @@ def rank_program(g, core, T, topo):
     aff(cs("RPH", 0, 143), cs("RP", 0, 143), 0.5, 0)
     aff(cs("RP16", 0, 143), cs("RP", 0, 143), 1.0 / 16, 0)
     aff(A("R1F"), red("RP", 1), 1, 0)
-    ts(A("LO"), A("LI"), C("lo"), ADD)
     prio[0] = 7
-    iota(A("T6"), [[1, 2], [2, 4], [0, 2]], 0, 0)
-    iota(A("T5"), [[16, 2], [256, 8]], 0, 1)
-    iota(A("T7"), [[-16, 2], [V, 8]], V + 31, -1)
-    iota(A("T8"), [[-16, 2], [0, 4], [1, 32]], 0, 0)
 
     def refill():
         for a in range(1, 9):
@@ -442,9 +460,11 @@ def rank_program(g, core, T, topo):
 
     refill()
     iota(WI, [[1, WW]], 0, 0)
+    held = range(len(ops), len(ops) + 4)
     ts(A("LC"), A("T7"), C("pd16"), ADD)
     ts(A("MASK"), A("T8"), C("pm"), GT)
     cp(A("LH"), A("T6"))
+    ts(A("LQ"), A("T5"), C("pd16"), ADD)
     ts(A("DJ"), cs("LI", 0, 8), C("lo"), ADD, float(V + FL), ADD)
     cp(cs("JZ1", 0, 8), cs("RP", 0, 8))
     tt(cs("JZ1", 8, 143), cs("RP", 8, 143), cs("RP", 0, 135), ADD)
@@ -482,7 +502,6 @@ def rank_program(g, core, T, topo):
     iota(A("ON8"), [[0, 1024]], 1, 0)
     asel(A("RG"), A("ON8"), [[-16, 8], [0, 8], [-1, 16]], EQo, 0, 1)
     asel(M("PERM"), cs("ON8", 0, 128), [[-1, 16], [-16, 8]], EQo, 0, 1)
-    ts(A("LQ"), A("T5"), C("pd16"), ADD)
     ts(M("V2"), A("QK"), 5.0, LT, 16.0, MUL)
     tt(A("OQ"), M("V2"), A("QK"), ADD)
     ts(C("t4"), C("pm"), 5.0, LT, 16.0, MUL)
@@ -492,6 +511,12 @@ def rank_program(g, core, T, topo):
     tt(M("TA1"), M("TC"), M("IB"), SUB)
     aff(C("bb1"), C("o1"), -BIG, 5 * BIG)
     aff(C("bc1"), C("o1"), -BIG, 4 * BIG - FL)
+    if TW:
+        aff(C("bbh1"), C("o1"), -BIG / 2, 2 * BIG)
+        aff(C("bch1"), C("o1"), -BIG / 2, BIG - FL)
+        aff(M("TAh1"), M("TA1"), 0.5, 0)
+
+    mark = {}
 
     def copy(out, a, key=None):
         either(lambda: cp(out, a), lambda: act(out, a, ACT.Copy), key)
@@ -507,16 +532,21 @@ def rank_program(g, core, T, topo):
         if t == 0:
             for i, q in enumerate([R] + others):
                 bank = 4 + i % 4
+                prio[0] = PR["win"] + 0.05 * i
                 for vh in range(8):
                     mm(B(bank, 64 * vh, 64 * vh + 64), cs("REP", 128 * vh, 128 * vh + 128), A("L", al, q))
                 wcopy(i + 10, q, bank)
-                for h in range(2):
-                    ts(A("L2", al, al, 8 * (1 - q // 4) + 2 * (q % 4) + h), A("L", al, q), C("hb" if h else "h0"), MUL)
+                prio[0] = PR["l2"]
+                cp(A("L2", al, 1 - q // 4, al, q % 4), A("L", al, q))
             for X in range(2):
                 prio[0] = PR["off"] if X == 0 else PR["pc"]
                 for b in range(4):
-                    mm(B(3 - 2 * X, b, 256, 4), A("L2", al, b, slice(8 * X, 8 * X + 8)), cs("MV", 0, 64))
+                    for h in range(2):
+                        ph = slice(64 * h, 64 * h + 64)
+                        mm(A("B%d" % (3 - 2 * X), ph, slice(b, 256, 4)), A("L2", ph, X, b), A("M", ph, ph))
                 ts(hf("OFF", X), B(3 - 2 * X, 0, 256), float(-FL), ADD)
+            for i in held:
+                ops[i]["after"].add(len(ops) - 1)
         else:
             for h in range(2):
                 either(lambda: ts(hf("P16", h), hf("P32", h), float(-H), ADD), lambda: aff(hf("P16", h), hf("P32", h), 1, -H))
@@ -524,23 +554,26 @@ def rank_program(g, core, T, topo):
                 prio[0] = PR["win"] + 0.05 * i
                 mm(B(4 + i % 4), cs("RG", 128 * q, 128 * q + 128), A("P16"))
                 wcopy(i, q, 4 + i % 4)
+                mark["W%d" % i] = len(ops) - 1
             for X in range(2):
                 prio[0] = PR["off"] if X == 0 else PR["qB"]
                 copy(hf("Q16", X), ind(sub(X), A("LQ")), "Q%d" % X)
+                mark["Q%d" % X] = len(ops) - 1
                 prio[0] = PR["off"]
                 for b in range(2):
                     mm(B(3 + 4 * X, b, 256, 2), cs("Q16", 256 * X + 128 * b, 256 * X + 128 * b + 128), M("PERM"))
                 ts(hf("OFF", X), B(3 + 4 * X, 0, 256), float(-FL), ADD)
+                mark["O%d" % X] = len(ops) - 1
         for X in range(2):
             prio[0] = PR["pcB" if X else "pc"]
-            copy(hf("PC", X), ind(sub(X), A("LP")), "PC%d" % X)
+            for h in range(2 if t else 0):
+                dma("s", A("PC", slice(64 * h, 64 * h + 64), slice(256 * X, 256 * X + 256)),
+                    A("P16", slice(64 - 64 * X, 128 - 64 * X), slice(256 * h, 256 * h + 256)), "pd%d" % X)
             either(lambda: ts(hf("NF", X), hf("PC", X), float(H), EQo),
                    lambda: act(hf("NF", X), hf("PC", X), ACT.Relu, bias=float(1 - H)), "NF%d" % X)
-        if t == 0:
-            prio[0] = 4
-            act(cs("P32", 0, V), ind(WN, A("LO")), ACT.Copy, bias=float(H))
+            mark["N%d" % X] = len(ops) - 1
 
-    ring = [0, 0]
+    ring, gat = [0, 0], []
 
     def complaints(X):
         prio[0] = PR["cB" if X else "cA"]
@@ -554,6 +587,7 @@ def rank_program(g, core, T, topo):
                 prio[0] = PR["gB" if X else "gA"]
                 n = GL[X][kk]
                 act(cs("S", s0, s0 + V * n), ind(WN, cs("OFF", s0 // 16, s0 // 16 + 32 * n)), ACT.Copy)
+                gat.append(len(ops) - 1)
             prio[0] = PR["cB" if X else "cA"]
             if c == 1:
                 for i in range(2):
@@ -578,13 +612,18 @@ def rank_program(g, core, T, topo):
         U1, U2 = (4, 5) if X == 0 else (0, 1)
         pc, nv, two, rb, rc, ge = (hf(nm, X) for nm in ("PC", "NV", "TWO", "RB", "RC", "GE"))
         act(nv, B(2 + X, 0, 256), ACT.Sign)
-        tt(two, B(6 + X, 0, 256), nv, MIN)
+        hh = "h" if WHO.get("TW%d" % X) == "a" else ""
+        if hh:
+            mm(B(6 + X, 0, 256), M("I64"), nv, False)
+            act(two, B(6 + X, 0, 256), ACT.Sign, bias=C("n64"))
+        else:
+            tt(two, B(6 + X, 0, 256), nv, MIN)
         for bank, m0 in ((U1, "I"), (U2, "SHF")):
             mm(B(bank, 0, 256), M(m0), pc)
-            mm(B(bank, 0, 256), M("TA%d" % t), two, False)
+            mm(B(bank, 0, 256), M("TA%s%d" % (hh, t)), two, False)
         mm(B(U2, 0, 256), M("IB"), nv, False)
-        ts(rb, B(U1, 0, 256), C("bb%d" % t), ADD, float(FL), MAX)
-        act(rc, B(U2, 0, 256), ACT.Relu, bias=C("bc%d" % t))
+        ts(rb, B(U1, 0, 256), C("bb%s%d" % (hh, t)), ADD, float(FL), MAX)
+        act(rc, B(U2, 0, 256), ACT.Relu, bias=C("bc%s%d" % (hh, t)))
         mm(B(U1, 256, 512), M("BD"), rb)
         gs = cs("GS", X, X + 1)
         act(ge, B(U1, 256, 512), ACT.Sign, bias=C("thr"), acc=gs)
@@ -639,59 +678,65 @@ def rank_program(g, core, T, topo):
                ind(cs("TS", 16 * X, 16 * X + 8), cs("LH", 8 * h, 8 * h + 8)), cs("BZ", 256 * X + 128, 256 * X + 256), EQo)
         scan(hf("DUP", X), hf("ED", X), A("MASK"), MAX, MIN)
 
-    def judge(X, p0, n, nmax, acc, pz, pb, dif, qb):
-        nu = n // 32
-        reps, first = 16 // nu, p0 + n == 128
+    def judge(X, p0, n, parts, acc, qb):
+        first = p0 + n == 128
         tag = "%d" % (X if first else 2)
-        lo, hi = 2048 * X + 16 * p0, 2048 * X + 16 * (p0 + n)
         g0 = 128 * X + p0
 
         def part(name):
             return cs(name, g0, g0 + n)
-        xz, xb = (cs("XZB", 256 * X + 128 * z + p0, 256 * X + 128 * z + p0 + n) for z in range(2))
+
+        def xzb(z, p, m):
+            return cs("XZB", 256 * X + 128 * z + p, 256 * X + 128 * z + p + m)
         prio[0] = PR["pat" + tag]
-        mm(B(acc, 0, 264), M("ZERO"), cs("W16", 0, 264))
+        mm(B(acc, 0, n), M("NBD"), xzb(0, p0, n))
         if first:
             prio[0] = PR["so%d" % X]
             mm(B(acc, 256, 264), A("I32M"), cs("TS", 16 * X, 16 * X + 8), False)
             for h in range(2):
                 e0 = 256 * X + 128 * h
                 mm(B(acc, 256 + h, 264, 2), M("IB"), cs("DUP", e0 + 31, e0 + 128, 32), False)
-        prio[0] = PR["pat" + tag]
-        for bank, x in ((pz, xz), (pb, xb))[:2 if nmax else 1]:
-            for i in range(reps):
-                mm(B(bank, i, 512, reps), M("I"), x)
         prio[0] = PR["sum" + tag]
+        mm(B(acc, n, 2 * n), M("NBD"), xzb(0, p0, n), False)
         for ih in range(2):
             reg = B(acc, n * ih, n * ih + n)
-            mm(reg, M("NBD"), xz, False)
-            if nmax:
-                mm(reg, M("LO%d" % (0 if nmax == nu else 1)), xb, False)
             mm(reg, M("NHI"), part("M0"), False)
             mm(reg, M("N%d" % ih), part("NFE"), False)
-        for q in range(nu):
-            bymax = q < nmax
-            xe = cs("XE", lo + q, hi, nu)
-            ks = [q + nu * j for j in range(reps)]
-            regs = [B(acc, n * (k // 8), n * (k // 8) + n) for k in ks]
-            for j, k in enumerate(ks):
-                mm(regs[j], red("JE", 8 + k % 8) if bymax else red("JE2", k % 8), cs("XE", lo + k, hi, 16), False)
-            for z in range(2):
-                m0 = V * (ring[1] % 8)
-                ring[1] += 1
-                prio[0] = PR["max" + tag]
-                if z == 0 or bymax:
-                    tt(cs("MM", m0, m0 + V), xe, B(pb if z else pz), MAX)
-                else:
-                    prio[0] = PR["dif" + tag]
-                    d = dif[q % len(dif)]
-                    mm(B(d), M("I"), xe)
-                    for i in range(reps):
-                        mm(B(d, i, 512, reps), M("NI"), xb, False)
-                    act(cs("MM", m0, m0 + V), B(d), ACT.Abs)
-                prio[0] = PR["sum" + tag]
+        for p, nmax, pz, pb, spare in parts:
+            dif = (pb, spare) if nmax == 0 else (spare,)
+            lo, hi = 2048 * X + 16 * p, 2048 * X + 16 * p + 1024
+            xz, xb = xzb(0, p, 64), xzb(1, p, 64)
+            prio[0] = PR["pat" + tag]
+            for bank, x in ((pz, xz), (pb, xb))[:2 if nmax else 1]:
+                for i in range(8):
+                    mm(B(bank, i, 512, 8), M("I"), x)
+            prio[0] = PR["sum" + tag]
+            for ih in range(2 if nmax else 0):
+                mm(B(acc, n * ih + p - p0, n * ih + p - p0 + 64), M("LO%d" % (2 - nmax)), xb, False)
+            for q in range(2):
+                bymax = q < nmax
+                xe = cs("XE", lo + q, hi, 2)
+                ks = range(q, 16, 2)
+                regs = [B(acc, n * (k // 8) + p - p0, n * (k // 8) + p - p0 + 64) for k in ks]
+                prio[0] = PR["je" + tag]
                 for j, k in enumerate(ks):
-                    mm(regs[j], red("JZ" if z == 0 else "JB" if bymax else "JE", k % 8), cs("MM", m0 + j, m0 + V, reps), False)
+                    mm(regs[j], red("JE", 8 + k % 8) if bymax else red("JE2", k % 8), cs("XE", lo + k, hi, 16), False)
+                for z in range(2):
+                    m0 = V * (ring[1] % 8)
+                    ring[1] += 1
+                    prio[0] = PR["max" + tag]
+                    if z == 0 or bymax:
+                        tt(cs("MM", m0, m0 + V), xe, B(pb if z else pz), MAX)
+                    else:
+                        prio[0] = PR["dif" + tag]
+                        d = dif[q % len(dif)]
+                        mm(B(d), M("I"), xe)
+                        for i in range(8):
+                            mm(B(d, i, 512, 8), M("NI"), xb, False)
+                        act(cs("MM", m0, m0 + V), B(d), ACT.Abs)
+                    prio[0] = PR["sum" + tag]
+                    for j, k in enumerate(ks):
+                        mm(regs[j], red("JZ" if z == 0 else "JB" if bymax else "JE", k % 8), cs("MM", m0 + j, m0 + V, 8), False)
         o1, o2 = B(qb, 0, n), B(qb, n, 2 * n)
         prio[0] = PR["fin" + tag]
         mm(o1, M("I"), cs("BZ", 256 * X + p0, 256 * X + p0 + n))
@@ -713,14 +758,21 @@ def rank_program(g, core, T, topo):
     for t in range(RO):
         window(t)
         complaints(0)
+        mark["g0"], mark["g1"] = gat[-len(GL[0])], gat[1 - len(GL[0])]
+        for a, b in (FIRST if t else FIRST0):
+            ops[mark[b]]["after"].add(mark[a])
         middle(t, 0)
         prepare(0)
+        if t == 0:
+            prio[0] = 4
+            aff(cs("P32", 0, V), A("P16"), 1, H)
+            ops[-1]["after"].add(gat[-1])
         complaints(1)
         middle(t, 1)
-        judge(0, 0, 128, NMAX[0], 2, 4, 5, (5, 6) if NMAX[0] == 0 else (6,), 6)
+        judge(0, 0, 128, [(64, NMAX[0], 4, 5, 6), (0, NMAX[1], 4, 5, 6)], 2, 6)
         prepare(1)
-        judge(1, 64, 64, NMAX[1], 3, 0, 1, (1, 7) if NMAX[1] == 0 else (7,), 7)
-        judge(1, 0, 64, NMAX[2], 2, 4, 5, (5, 6) if NMAX[2] == 0 else (6,), 6)
+        judge(1, 64, 64, [(64, NMAX[2], 0, 1, 7)], 3, 7)
+        judge(1, 0, 64, [(0, NMAX[3], 4, 5, 6)], 2, 6)
 
     prio[0] = 0
     dma("s", A("YS"), cs("P32", 0, V), "ys")
@@ -739,13 +791,14 @@ def rank_program(g, core, T, topo):
         o["pre"] = set(o["after"])
         for d in o["deps"]:
             o["pre"].update(bysem[ops[d]["sem"]] if ops[d]["sem"] is not None else [d])
-        o["left"], o["ready"] = len(o["pre"]), 0.0
+        o["left"], o["ready"], o["tail"] = len(o["pre"]), 0.0, 0.0
         for d in o["pre"]:
             users[d].append(i)
-    for i in reversed(range(len(ops))):
-        o = ops[i]
-        c = min(o["cost"].values()) if o["eng"] == "?" else min(o["cost"], 20.0)
-        o["tail"] = c + max([0.0] + [ops[u]["tail"] + 0.1 for u in users[i]])
+    for _ in range(2):
+        for i in reversed(range(len(ops))):
+            o = ops[i]
+            c = min(o["cost"].values()) if o["eng"] == "?" else min(o["cost"], 20.0)
+            o["tail"] = c + max([0.0] + [ops[u]["tail"] + 0.1 for u in users[i]])
     free = {e: 0.0 for e in list(queue) + ["x"]}
     ready = {e: [] for e in free}
 

import numpy as np
from concourse.bass import DstId, RemoteDMATransfer
from concourse.mybir import AluOpType as ALU
from concourse.mybir import ActivationFunctionType as ACT

N, V, W, RO = 8, 512, 4096, 2
H = 2048
O = 8
FL = -(H + O)
BIG = 8192.0
NONE = W + O + 300
WW = NONE + 12
NMAX = (2, 0, 2, 0)
ARR = (9.5, 10.5, 10.55, 10.6, 10.65, 11.4, 11.45)
FIRST = (("Q0", "W5"), ("O0", "Q1"), ("g0", "N1"))
FIRST0 = (("g0", "N1"),)

WHO = dict(Q1="v", W1="v", W3="v", W7="v", XZ1="v", XE13="v", W10="v", W11="v", W16="v",
           NF1="a", CC1="a", XZ0="a", XE01="a", XE02="a", XE03="a", XE10="a", XE11="a", E0="a",
           BZ1="a", W0="a", W2="a", W4="a", W6="a", W17="a", NE0="a", NE1="a")
G1 = {k: 1 for k in range(8)}
GL = (G1, G1)
SHY, TAILW, SLACK = 0.5, 0.001, 0.05
PR = dict(l2=1, win=1, off=-3, pc=4.5, pcB=-3, qB=-2, gA=-3, gB=4.5, cA=-4, cB=-1, red=-3, mid=-4, mB=-3,
          xe=2, xB=-2, xz0=1, xz1=-2, prep=2, pB=-3, so0=-2, so1=0,
          pat0=0, pat1=-1, pat2=-4, max0=4, max1=-3, max2=4, dif0=-3, dif1=-3, dif2=-3,
          je0=0, je1=-1, je2=-3, sum0=-3, sum1=-4, sum2=4.5, fin0=-1, fin1=4.5, fin2=4.5)

F32, BF, F16, I32, U16 = "float32", "bfloat16", "float16", "int32", "uint16"
SCRATCH = {}


def _sb(names, cols, dtype):
    for nm in names.split():
        SCRATCH[nm] = ("sbuf", [128] + (cols if isinstance(cols, list) else [cols]), dtype)


_sb("SA", [8, 4, 16], I32)
_sb("SH L", [8, 4, 16], F16)
_sb("L2", [2, 4, 4, 16], F16)
_sb("WN WI", WW, F32)
_sb("WX", WW, BF)
_sb("OFF", 512, U16)
_sb("S", 8192, F16)
_sb("EQ", 3072, BF)
_sb("P16 Q16 PC RB U G BZ", 512, F16)
_sb("W16", 1024, F16)
_sb("P32", 768, F32)
_sb("NF NV TWO GE XZB ED FF DUP", 512, BF)
_sb("RC VALS CC", 512, F32)
_sb("VI", 256, F32)
_sb("CW", 9 * V, F32)
_sb("LI", 32, I32)
_sb("T5 T6 T7", 16, I32)
_sb("OT OB LO", 32, U16)
_sb("LP LQ LH LC SO", 16, U16)
_sb("TS", 32, F32)
_sb("Z3 SO1 OH SEL SE2", 16, F32)
_sb("DJ GS", 8, F32)
_sb("OE", 256, U16)
_sb("E32 G1 NEW", 256, F32)
_sb("M0 NFE ZR ONES T8 MASK", 256, BF)
_sb("XE MM", 4096, BF)
_sb("PI", 8, I32)
_sb("C", 48, F32)
_sb("QD QK R0 OQ D2E", 128, BF)
_sb("DC", 128, F16)
_sb("I32M R1F", 128, F32)
_sb("J RP RPH RP16 JZ JZ1 JB JE JE2", 144, BF)
_sb("CB", 2048, BF)
_sb("REP RG ON8", 1024, BF)
_sb("M", 36 * 128, BF)
for _b in range(8):
    SCRATCH["B%d" % _b] = ("psum", [128, 512], F32)
SCRATCH["XS"] = ("dram", [8, 128, 64], BF)
SCRATCH["XR"] = ("dram", [8, 128, 64], BF)
SCRATCH["YS"] = ("dram", [8, 128, 64], F32)
SCRATCH["YR"] = ("dram", [8, 128, 64], F32)

SEMAPHORES = (["cv", "ca", "ct", "cg", "sent", "ld", "xs", "x0", "x1", "xa", "ys", "yo", "pc0", "pc1", "pd0", "pd1", "p16"]
              + ["sa%d" % i for i in range(N)] + ["ya%d" % i for i in range(N)])

MATS = ["I", "BD", "SHF", "IS", "TA0", "TA1", "TAh0", "TAh1", "I64", "TC", "D2", "K5", "PERM", "IB", "NBD", "LO0", "LO1",
        "NHI", "N0", "N1", "M10", "M11", "M20", "M21", "BDB", "BD4", "NI", "NO", "G1", "G2", "V1", "V2", "V3"]
COLS = ["p", "pd", "g4", "hb", "pm", "pd16", "wb0", "wb1", "o1", "bb0", "bb1", "bc0", "bc1", "bbh0", "bbh1", "bch0", "bch1",
        "n64", "thr", "vb", "lp", "lo", "xo", "shf", "up", "dn", "d0", "dm", "dp", "le9", "k5", "ev", "s1", "s2", "w2",
        "t1", "t2", "t3", "t4", "t5"]


def plan(src, cores, topo):
    me = cores[src]
    others = [(src + d) % N for d in range(1, N)]
    near = [q for q in others if topo.chip(cores[q]) == topo.chip(me)]
    far = [q for q in others if q not in near]

    def way(q):
        a, b = topo.chip(me), topo.chip(cores[q])
        return (topo.mates(a, b) or topo.same_plane(a, b), topo.die(cores[q]) == topo.die(me))
    far.sort(key=way)
    out = topo.engines(me, cores[far[0]])
    first, second = far[:4], far[4:]
    calls = [[], []]
    n1, n2 = len(out) // len(first), len(out) // len(second)
    for i, q in enumerate(first):
        calls[0].append((q, out[i * n1:(i + 1) * n1]))
    for i, q in enumerate(second):
        calls[1].append((q, out[i * n2:(i + 1) * n2]))
    for i, q in enumerate(near):
        free = [e for e in topo.engines(me, cores[q]) if e not in out]
        calls[0].append((q, free[i * n1:(i + 1) * n1]))
    return calls


def rank_program(g, core, T, topo):
    R = T.rank_of(core)
    if R is None:
        return
    cores = list(T.cores)
    queue = {"v": g.vector, "a": g.scalar, "t": g.tensor, "g": g, "s": g.sync}
    csem = {"v": "cv", "a": "ca", "t": "ct", "g": "cg"}
    ops, hist, total, flat, last, group, pair, prio = [], {}, {}, {}, {}, {}, [], [0]

    def A(name, *idx):
        if name not in SCRATCH:
            return {"ap": T[name][idx], "reg": [], "n": 0, "dt": None, "ps": False}
        where, shape, dtype = SCRATCH[name]
        if len(idx) == 0:
            idx = (slice(None),)
        n = 0
        if where != "dram":
            if name not in flat:
                flat[name] = np.arange(int(np.prod(shape[1:]))).reshape(shape[1:])
            f = flat[name][idx[1:]] if len(idx) > 1 else flat[name]
            lo, hi, n = int(np.min(f)), int(np.max(f)) + 1, int(np.size(f))
        if where == "dram" and isinstance(idx[0], int):
            lo, hi = idx[0], idx[0] + 1
        elif where != "sbuf":
            lo, hi = 0, 1 << 30
        return {"ap": T[name][idx], "reg": [(name, lo, hi)], "n": n, "dt": dtype, "ps": where == "psum"}

    al = slice(None)

    def cs(name, lo, hi, step=1):
        return A(name, al, slice(lo, hi, step) if step != 1 else slice(lo, hi))

    def ind(win, off):
        return {"ap": win["ap"].indirect(off["ap"]), "reg": win["reg"], "off": off["reg"], "n": 16 * off["n"],
                "dt": win["dt"], "ps": False}

    def val(x):
        return x["ap"] if isinstance(x, dict) else x

    def either(on_vector, on_scalar, key=None):
        if key in WHO:
            return on_scalar() if WHO[key] == "a" else on_vector()
        pair.append([])
        on_vector()
        on_scalar()
        (cv, outs, ins, tv), (ca, _, more, ta) = pair.pop()
        rec("?", {"v": cv, "a": ca}, outs, ins + more, {"v": tv, "a": ta})

    def rec(eng, call, outs, ins, cost, sem=None, inc=16, hold=None, acc=None):
        if pair:
            pair[-1].append((call, outs, ins, cost))
            return
        rd, wr = [], []
        for x in ins:
            if isinstance(x, dict):
                rd += x["reg"] + x.get("off", [])
        for x in outs:
            wr += x["reg"]
            rd += x.get("off", [])
        me = len(ops)
        deps, after = set(), set()
        for regs, isw in ((rd, False), (wr, True)):
            for nm, lo, hi in regs:
                ps = SCRATCH[nm][0] == "psum"
                for (l2, h2, o2, w2) in hist.get(nm, []):
                    if l2 < hi and lo < h2:
                        other = ops[o2]
                        same = other["eng"] == eng != "?" and other["sem"] is None and sem is None
                        if same and eng == "t":
                            if ps and not (other["acc"] is acc and acc["first"] != o2):
                                after.add(o2)
                            continue
                        if sem is not None and other["sem"] == sem:
                            continue
                        if isw or w2 or (ps and not same):
                            deps.add(o2)
        for regs, isw in ((rd, False), (wr, True)):
            for nm, lo, hi in regs:
                h = hist.setdefault(nm, [])
                if isw and sem is None and (acc is None or acc["first"] == me):
                    h[:] = [e for e in h if not (lo <= e[0] and e[1] <= hi)]
                h.append((lo, hi, me, isw))
        if sem is not None:
            total[sem] = total.get(sem, 0) + inc
        if eng != "x" and (eng == "g" or sem is not None):
            if eng in last:
                after.add(last[eng])
            last[eng] = me
        ops.append({"eng": eng, "call": call, "deps": deps, "after": after, "sem": sem, "sig": False, "n": 0,
                    "cost": cost, "hold": cost if hold is None else hold, "prio": prio[0], "acc": acc})

    CY = 0.00083

    def cost(out, ins, fix, twice=False):
        full = [x for x in [out] + ins if isinstance(x, dict) and x["n"] > 1]
        if "off" in out:
            return 0.05 + 3.8 * CY * out["n"]
        if any("off" in x for x in full):
            return 0.06 + 1.56 * CY * out["n"]
        m = 0.5 if fix < 0.05 and all(x["dt"] in (BF, F16, U16) for x in full) else 1.0
        return fix + CY * max(64, out["n"] * m * (2 if twice else 1))

    def ts(out, in0, s1, op0, s2=None, op1=None):
        if op1 is None:
            rec("v", lambda: g.vector.tensor_scalar(val(out), val(in0), val(s1), None, op0), [out], [in0, s1],
                cost(out, [in0], 0.03))
        else:
            rec("v", lambda: g.vector.tensor_scalar(val(out), val(in0), val(s1), val(s2), op0, op1), [out], [in0, s1, s2],
                cost(out, [in0], 0.03))

    def tt(out, a, b, op):
        rec("v", lambda: g.vector.tensor_tensor(val(out), val(a), val(b), op), [out], [a, b],
            cost(out, [a, b], 0.03, not (a["ps"] or b["ps"])))

    def cp(out, a):
        rec("v", lambda: g.vector.tensor_copy(val(out), val(a)), [out], [a], cost(out, [a], 0.03))

    def ms(out, c):
        rec("v", lambda: g.vector.memset(val(out), c), [out], [], cost(out, [], 0.03))

    def scan(out, a, b, op0, op1):
        rec("v", lambda: g.vector.tensor_tensor_scan(val(out), val(a), val(b), 0.0, op0, op1), [out], [a, b],
            cost(out, [a, b], 0.03))

    def act(out, a, func, bias=0.0, scale=1.0, acc=None):
        if acc is None:
            rec("a", lambda: g.scalar.activation(val(out), val(a), func, bias=val(bias), scale=val(scale)), [out],
                [a, bias, scale], cost(out, [a], 0.06))
        else:
            rec("a", lambda: g.scalar.activation(val(out), val(a), func, bias=val(bias), scale=val(scale),
                                                 accum_out=val(acc)), [out, acc], [a, bias, scale], cost(out, [a], 0.08))

    def mm(out, lhsT, rhs, start=True):
        bank = out["reg"][0][0]
        if start:
            group[bank] = {"first": len(ops), "left": 0}
        grp = group[bank]
        grp["left"] += 1

        def call():
            grp["left"] -= 1
            return g.tensor.matmul(val(out), val(lhsT), val(rhs), start, grp["left"] == 0)
        rec("t", call, [out], [lhsT, rhs], CY / 2 * max(64, out["n"]) * (4 if rhs["dt"] == F32 else 1), acc=grp)

    def iota(out, pat, base, cm):
        c = 0.13 + 2 * CY * out["n"]
        if out["dt"] != I32:
            rec("g", lambda: g.iota(val(out), pat, base, cm, allow_small_or_imprecise_dtypes=True), [out], [], c)
        else:
            rec("g", lambda: g.iota(val(out), pat, base, cm), [out], [], c)

    def asel(out, a, pat, op, base, cm, fill=0.0):
        rec("g", lambda: g.affine_select(val(out), val(a), pat, op, fill, base, cm), [out], [a], 0.17 + 2 * CY * out["n"])

    def dma(eng, out, a, sem):
        rec(eng, lambda: queue[eng].dma_start(val(out), val(a)).then_inc(T.sem[sem], 16), [out], [a], 2.0, sem=sem, hold=0.1)

    def send(src_of, dst, sem, keep=lambda q: True, engines=None):
        for call in plan(R, cores, topo):
            call = [(q, engines or e) for q, e in call if keep(q)]
            if not call:
                continue
            trs, n = [], 0
            for q, engs in call:
                rid, pid = topo.addr(cores[q])[:2]
                trs.append(RemoteDMATransfer(dst_ids=[DstId(rid=rid, pnc=pid)], dma_engine_mask=sum(1 << e for e in engs),
                                             remote_sem=T.sem[sem], src=src_of(q)["ap"], dst=dst["ap"]))
                n += len(engs)
            rec("g", lambda trs=trs: g.remote_dma_fused(trs, local_sem=T.sem["sent"]), [],
                [src_of(q) for q, _ in call], 1.2, sem="sent", inc=n)

    def arrive(q, out, sem, when, n=None):
        n = n or [len(e) for call in plan(q, cores, topo) for d, e in call if d == R][0]
        rec("x", None, [out], [], when, sem=sem, inc=n)

    def M(name):
        i = MATS.index(name)
        return cs("M", 128 * i, 128 * i + 128)

    def C(name):
        i = COLS.index(name)
        return cs("C", i, i + 1)

    def red(name, k):
        return cs(name, 15 - k, 143 - k)

    def B(i, lo=0, hi=512, step=1):
        return cs("B%d" % i, lo, hi, step)

    def hf(name, X, n=256):
        return cs(name, n * X, n * X + n)

    EQo, NE, GT, GE_, LT = ALU.is_equal, ALU.not_equal, ALU.is_gt, ALU.is_ge, ALU.is_lt
    ADD, SUB, MUL, MAX, MIN = ALU.add, ALU.subtract, ALU.mult, ALU.max, ALU.min
    WN, WX, WI = A("WN"), A("WX"), A("WI")

    def OH(l):
        return cs("OH", l, l + 1)

    def ln(out, col, w):
        ts(out, cs("J", 15, 15 + out["n"]), col, EQo, w, MUL)

    def sel(out, a, ap, ax, ak, d, op, fill=0.0):
        asel(M(out), M(a), [[ax, 8], [ak, 16]], op, d, ap, fill)

    def diag(out, a, d, fill):
        sel(out, a, -1, 16, 1, -d, NE, fill)

    def line(out, a, d):
        sel(out, a, -1, 16, 1, -d, EQo)

    def rows(out, a, lo, hi, fill=0.0):
        if hi is None:
            sel(out, a, 1, -16, 0, -lo, GE_, fill)
        else:
            sel(out, a, -1, 16, 0, hi, GE_, fill)

    def aff(out, a, scale, bias):
        act(out, a, ACT.Copy, bias=float(bias), scale=float(scale))

    prio[0] = -9
    dma("a", A("XS"), A("x", al), "xs")
    for q in range(N):
        for h in range(2):
            dma("sa"[h], A("SA", slice(64 * h, 64 * h + 64), q),
                A("stars", slice(16 * q, 16 * q + 16), slice(256 * h, 256 * h + 256)), "ld")

    iota(cs("PI", 0, 1), [[0, 1]], 0, 1)
    iota(A("QD"), [[1, 8], [0, 16]], 0, 0)
    iota(A("QK"), [[0, 8], [1, 16]], 0, 0)
    iota(cs("J", 0, 143), [[1, 143]], -15, 0)
    iota(A("LI"), [[16, 32]], 0, 1)
    iota(A("VI"), [[1, 256]], 0, 0)

    ts(A("SH"), A("SA"), float(-H), ADD)
    near = [q for q in range(N) if topo.chip(cores[q]) == topo.chip(core)]
    send(lambda q: A("XS", q), A("XR", R), "xa", lambda q: q in near)
    send(lambda q: A("SH", al, q), A("L", al, R), "sa%d" % R)
    send(lambda q: A("XS", q), A("XR", R), "xa", lambda q: q not in near)
    iota(A("T8"), [[-16, 2], [0, 4], [1, 32]], 0, 0)
    iota(A("T6"), [[1, 2], [2, 4], [0, 2]], 0, 0)
    iota(A("T5"), [[16, 2], [256, 2], [V, 4]], 0, 1)
    iota(A("T7"), [[-16, 2], [V, 8]], V + 31, -1)
    ts(A("L", al, R), A("SA", al, R), float(-H), ADD)
    others = sorted((q for q in range(N) if q != R),
                    key=lambda q: (q not in near, R in [d for d, _ in plan(q, cores, topo)[1]]))
    for i, q in enumerate(others):
        arrive(q, A("L", al, q), "sa%d" % q, ARR[i])
        arrive(q, A("XR", q), "xa", 13.0)

    for q in sorted([R] + others, key=lambda q: q < 4):
        for h in range(2):
            p0, X = 64 * h + 16 * (q % 4), 1 - q // 4
            dma("s", A("PC", slice(p0, p0 + 16), slice(256 * X, 256 * X + 256)), A("L", slice(64 * h, 64 * h + 64), q), "pc%d" % X)
    for q in range(N):
        for h in range(2):
            dma("s", A("P16", slice(16 * q, 16 * q + 16), slice(256 * h, 256 * h + 256)), A("L", slice(64 * h, 64 * h + 64), q), "p16")

    for q in range(N):
        src = A("x", slice(16 * R, 16 * R + 16), al) if q == R else A("XR", q)
        dma("s", A("WX", slice(0, 16), slice(O + V * q, O + V * q + V)), src, "x0")
    for x in range(1, 8):
        dma("s", A("WX", slice(16 * x, 16 * x + 16), slice(O, O + W)), A("WX", slice(0, 16), slice(O, O + W)), "x1")

    prio[0] = 5
    for i, (sh, m) in enumerate(((4, 7), (4, 3), (6, 1))):
        ts(cs("PI", i + 1, i + 2), cs("PI", 0, 1), sh, ALU.arith_shift_right, m, ALU.bitwise_and)
    cp(cs("C", 0, 4), cs("PI", 0, 4))
    ms(cs("WN", 0, O), float(H))
    ms(cs("WN", W + O, WW), float(H))
    ms(cs("WX", 0, O), 0.0)
    ms(cs("WX", W + O, WW), 0.0)
    ts(C("pd16"), C("pd"), 16.0, MUL)
    ts(M("BD"), A("QD"), C("pd"), EQo)
    tt(C("pm"), C("p"), C("pd16"), SUB)
    ts(A("OH"), cs("QK", 0, 16), C("pm"), EQo)
    ts(cs("RP", 0, 143), cs("J", 0, 143), C("pd16"), EQo)
    ts(A("R0"), A("QK"), -4.0, MUL, C("p"), ADD)
    for vh in range(8):
        ts(cs("REP", 128 * vh, 128 * vh + 128), A("R0"), float(64 * (vh // 4) + vh % 4), EQo)
    ts(C("t1"), C("g4"), 2.0, MUL, C("hb"), ADD)
    aff(C("ev"), C("hb"), -1, 1)
    aff(C("lo"), C("pd"), 496, O)
    for X in range(2):
        aff(C("wb%d" % X), C("t1"), 256, -H * X)
    for l in range(16):
        l = (l + 1) % 16
        act(cs("CB", 128 * l, 128 * l + 128), M("BD"), ACT.Identity, scale=OH(l))
    for i in range(4):
        act(cs("W16", 256 * i, 256 * i + 256), A("VI"), ACT.Identity, bias=C("wb%d" % (i // 2)))
    ln(M("I"), C("p"), 1.0)
    ts(C("t5"), OH(0), 16.0, MUL, -1.0, ADD)
    tt(C("shf"), C("t5"), C("p"), ADD)
    ln(M("SHF"), C("shf"), 1.0)
    tt(M("IS"), M("SHF"), M("I"), ADD)
    prio[0] = 6
    ln(M("IB"), C("p"), BIG)
    ts(M("V1"), A("QK"), C("pm"), GT, BIG, MUL)
    tt(M("TC"), M("V1"), M("BD"), MUL)
    tt(M("TA0"), M("TC"), M("IB"), SUB)
    aff(C("bb0"), C("pm"), -BIG, 0)
    aff(C("bc0"), C("pm"), -BIG, -BIG - FL)
    TW = "a" in (WHO.get("TW0"), WHO.get("TW1"))
    if TW:
        aff(C("bbh0"), C("pm"), -BIG / 2, -BIG / 2)
        aff(C("bch0"), C("pm"), -BIG / 2, -1.5 * BIG - FL)
        aff(M("TAh0"), M("TA0"), 0.5, 0)
        aff(M("I64"), M("I"), 64, 0)
        ms(C("n64"), -64.5)
    aff(C("t2"), C("pm"), -V, V + H - 15 * FL + 0.5)
    aff(C("up"), C("p"), 1, 1)
    aff(C("dn"), C("p"), 1, -1)
    aff(C("s2"), C("g4"), 1, 8)
    aff(C("w2"), OH(1), -1024, 0)
    aff(C("xo"), C("pd"), -V, H)
    ts(C("t3"), OH(0), 1.0e6, MUL, C("t2"), ADD)
    ts(C("t4"), C("pm"), 8.5, GT, -1.0e6, MUL)
    tt(C("thr"), C("t3"), C("t4"), ADD)
    ts(C("le9"), C("pm"), 9.5, LT)
    ts(C("dp"), C("pm"), 8.5, LT, -0.5, MUL)
    ts(C("dm"), C("le9"), OH(0), SUB, -0.5, MUL)
    ts(C("d0"), C("dm"), C("dp"), ADD, -1.0, MUL)
    aff(C("k5"), C("le9"), V, 0)
    ln(M("V1"), C("p"), C("d0"))
    ln(M("V2"), C("dn"), C("dm"))
    ln(M("V3"), C("up"), C("dp"))
    tt(M("V1"), M("V1"), M("V2"), ADD)
    tt(M("D2"), M("V1"), M("V3"), ADD)
    ln(M("K5"), C("p"), C("k5"))
    ms(cs("D2E", 0, 64), 0.0)
    ts(cs("D2E", 64, 128), cs("M", 128 * MATS.index("D2"), 128 * MATS.index("D2") + 64), C("ev"), MUL)
    ts(C("vb"), OH(0), float(-16 * FL), MUL, -NONE / 2, ADD)
    ts(C("s1"), C("pm"), 4.0, MUL, C("g4"), ADD)
    ln(cs("SEL", 0, 12), C("s1"), 1.0)
    ln(cs("SE2", 0, 12), C("s2"), C("w2"))
    tt(cs("SEL", 0, 12), cs("SEL", 0, 12), cs("SE2", 0, 12), ADD)
    ms(A("ZR"), 0.0)
    ms(A("ONES"), 1.0)
    aff(cs("RPH", 0, 143), cs("RP", 0, 143), 0.5, 0)
    aff(cs("RP16", 0, 143), cs("RP", 0, 143), 1.0 / 16, 0)
    aff(A("R1F"), red("RP", 1), 1, 0)
    prio[0] = 7

    def refill():
        for a in range(1, 9):
            iota(cs("CW", V * a, V * a + 32), [[0, 32]], NONE // 2, 0)

    refill()
    iota(WI, [[1, WW]], 0, 0)
    held = range(len(ops), len(ops) + 4)
    ts(A("LC"), A("T7"), C("pd16"), ADD)
    ts(A("MASK"), A("T8"), C("pm"), GT)
    cp(A("LH"), A("T6"))
    ts(A("LQ"), A("T5"), C("pd16"), ADD)
    ts(A("DJ"), cs("LI", 0, 8), C("lo"), ADD, float(V + FL), ADD)
    cp(cs("JZ1", 0, 8), cs("RP", 0, 8))
    tt(cs("JZ1", 8, 143), cs("RP", 8, 143), cs("RP", 0, 135), ADD)
    aff(cs("JB", 0, 143), cs("RP", 0, 143), -2, 0)
    aff(cs("JE", 0, 143), cs("RP", 0, 143), -1, 0)
    aff(cs("JZ", 0, 143), cs("JZ1", 0, 143), 2, 0)
    aff(cs("JE2", 0, 143), cs("JZ1", 0, 143), -1, 0)
    aff(A("I32M"), M("I"), 1, 0)
    aff(M("NI"), M("I"), -1, 0)
    aff(M("NO"), M("I"), BIG + H, 0)
    aff(M("NBD"), M("BD"), -1, 0)
    aff(M("BDB"), M("BD"), BIG, 0)
    aff(M("BD4"), M("BD"), W, 0)
    sel("LO0", "BD", 0, 0, -1, 8, GT)
    asel(M("LO1"), M("LO0"), [[0, 64], [-1, 2]], GT, 1, 0)
    sel("NHI", "NBD", 0, 0, 1, -8, GE_)
    diag("G1", "IB", 8, BIG)
    rows("G2", "G1", 0, None)
    rows("N0", "G2", None, 7)
    diag("G1", "IB", -8, BIG)
    rows("G2", "G1", 8, None)
    rows("N1", "G2", None, 15)
    for nm, d in (("M10", 0), ("M11", 8)):
        line("G1", "BD4", d)
        rows("G2", "G1", None, 7, -BIG)
        rows(nm, "G2", None, 15)
    rows("G1", "TA0", None, 7, BIG)
    rows("M20", "G1", None, 15)
    sel("G1", "BDB", -1, 16, 1, -8, GT)
    diag("G2", "G1", 8, -BIG)
    rows("G1", "G2", 0, None)
    rows("G2", "G1", None, 7, BIG)
    rows("M21", "G2", None, 15)
    prio[0] = 8
    iota(A("ON8"), [[0, 1024]], 1, 0)
    asel(A("RG"), A("ON8"), [[-16, 8], [0, 8], [-1, 16]], EQo, 0, 1)
    asel(M("PERM"), cs("ON8", 0, 128), [[-1, 16], [-16, 8]], EQo, 0, 1)
    ts(M("V2"), A("QK"), 5.0, LT, 16.0, MUL)
    tt(A("OQ"), M("V2"), A("QK"), ADD)
    ts(C("t4"), C("pm"), 5.0, LT, 16.0, MUL)
    tt(C("o1"), C("t4"), C("pm"), ADD)
    ts(M("V2"), A("OQ"), C("o1"), GT, BIG, MUL)
    tt(M("TC"), M("V2"), M("BD"), MUL)
    tt(M("TA1"), M("TC"), M("IB"), SUB)
    aff(C("bb1"), C("o1"), -BIG, 5 * BIG)
    aff(C("bc1"), C("o1"), -BIG, 4 * BIG - FL)
    if TW:
        aff(C("bbh1"), C("o1"), -BIG / 2, 2 * BIG)
        aff(C("bch1"), C("o1"), -BIG / 2, BIG - FL)
        aff(M("TAh1"), M("TA1"), 0.5, 0)

    mark = {}

    def copy(out, a, key=None):
        either(lambda: cp(out, a), lambda: act(out, a, ACT.Copy), key)

    def wcopy(i, q, bank):
        copy(cs("WN", O + V * q, O + V * q + V), B(bank), "W%d" % i)

    def sub(X):
        return cs("WN", O + H * (1 - X), O + H * (2 - X))

    def window(t):
        prio[0] = PR["win"]
        if t == 0:
            for i, q in enumerate([R] + others):
                bank = 4 + i % 4
                prio[0] = PR["win"] + 0.05 * i
                for vh in range(8):
                    mm(B(bank, 64 * vh, 64 * vh + 64), cs("REP", 128 * vh, 128 * vh + 128), A("L", al, q))
                wcopy(i + 10, q, bank)
                prio[0] = PR["l2"]
                cp(A("L2", al, 1 - q // 4, al, q % 4), A("L", al, q))
            for X in range(2):
                prio[0] = PR["off"] if X == 0 else PR["pc"]
                for b in range(4):
                    for h in range(2):
                        ph = slice(64 * h, 64 * h + 64)
                        mm(A("B%d" % (3 - 2 * X), ph, slice(b, 256, 4)), A("L2", ph, X, b), A("M", ph, ph))
                ts(hf("OFF", X), B(3 - 2 * X, 0, 256), float(-FL), ADD)
            for i in held:
                ops[i]["after"].add(len(ops) - 1)
        else:
            for h in range(2):
                either(lambda: ts(hf("P16", h), hf("P32", h), float(-H), ADD), lambda: aff(hf("P16", h), hf("P32", h), 1, -H))
            for i, q in enumerate((4, 5, 6, 7, 0, 1, 2, 3)):
                prio[0] = PR["win"] + 0.05 * i
                mm(B(4 + i % 4), cs("RG", 128 * q, 128 * q + 128), A("P16"))
                wcopy(i, q, 4 + i % 4)
                mark["W%d" % i] = len(ops) - 1
            for X in range(2):
                prio[0] = PR["off"] if X == 0 else PR["qB"]
                copy(hf("Q16", X), ind(sub(X), A("LQ")), "Q%d" % X)
                mark["Q%d" % X] = len(ops) - 1
                prio[0] = PR["off"]
                for b in range(2):
                    mm(B(3 + 4 * X, b, 256, 2), cs("Q16", 256 * X + 128 * b, 256 * X + 128 * b + 128), M("PERM"))
                ts(hf("OFF", X), B(3 + 4 * X, 0, 256), float(-FL), ADD)
                mark["O%d" % X] = len(ops) - 1
        for X in range(2):
            prio[0] = PR["pcB" if X else "pc"]
            for h in range(2 if t else 0):
                dma("s", A("PC", slice(64 * h, 64 * h + 64), slice(256 * X, 256 * X + 256)),
                    A("P16", slice(64 - 64 * X, 128 - 64 * X), slice(256 * h, 256 * h + 256)), "pd%d" % X)
            either(lambda: ts(hf("NF", X), hf("PC", X), float(H), EQo),
                   lambda: act(hf("NF", X), hf("PC", X), ACT.Relu, bias=float(1 - H)), "NF%d" % X)
            mark["N%d" % X] = len(ops) - 1

    ring, gat = [0, 0], []

    def complaints(X):
        prio[0] = PR["cB" if X else "cA"]
        cnt = (B(2 + X, 0, 256), B(6 + X, 0, 256))
        mm(cnt[0], M("I"), hf("NF", X))
        mm(cnt[1], M("IS"), hf("NF", X))

        def compare(kk, c):
            s0 = 4096 * X + V * kk
            if c == 0 and kk in GL[X]:
                prio[0] = PR["gB" if X else "gA"]
                n = GL[X][kk]
                act(cs("S", s0, s0 + V * n), ind(WN, cs("OFF", s0 // 16, s0 // 16 + 32 * n)), ACT.Copy)
                gat.append(len(ops) - 1)
            prio[0] = PR["cB" if X else "cA"]
            if c == 1:
                for i in range(2):
                    l = (2 * kk + i + 1) % 16
                    mm(B(kk % 2, 256 * i, 256 * i + 256), cs("CB", 128 * l, 128 * l + 128), hf("PC", X))
            e0 = V * (ring[0] % 6)
            ring[0] += 1
            tt(cs("EQ", e0, e0 + V), cs("S", s0, s0 + V), B(kk % 2) if c else hf("W16", X, 512), EQo)
            prio[0] = PR["red"]
            for i in range(2):
                mm(cnt[c], red("RP", 2 * kk + i), cs("EQ", e0 + 256 * i, e0 + 256 * i + 256), False)

        for kk in range(6):
            compare(kk, 0)
            compare(kk, 1)
        for c in range(2):
            compare(6, c)
            compare(7, c)

    def middle(t, X):
        prio[0] = PR["mB" if X else "mid"]
        U1, U2 = (4, 5) if X == 0 else (0, 1)
        pc, nv, two, rb, rc, ge = (hf(nm, X) for nm in ("PC", "NV", "TWO", "RB", "RC", "GE"))
        act(nv, B(2 + X, 0, 256), ACT.Sign)
        hh = "h" if WHO.get("TW%d" % X) == "a" else ""
        if hh:
            mm(B(6 + X, 0, 256), M("I64"), nv, False)
            act(two, B(6 + X, 0, 256), ACT.Sign, bias=C("n64"))
        else:
            tt(two, B(6 + X, 0, 256), nv, MIN)
        for bank, m0 in ((U1, "I"), (U2, "SHF")):
            mm(B(bank, 0, 256), M(m0), pc)
            mm(B(bank, 0, 256), M("TA%s%d" % (hh, t)), two, False)
        mm(B(U2, 0, 256), M("IB"), nv, False)
        ts(rb, B(U1, 0, 256), C("bb%s%d" % (hh, t)), ADD, float(FL), MAX)
        act(rc, B(U2, 0, 256), ACT.Relu, bias=C("bc%s%d" % (hh, t)))
        mm(B(U1, 256, 512), M("BD"), rb)
        gs = cs("GS", X, X + 1)
        act(ge, B(U1, 256, 512), ACT.Sign, bias=C("thr"), acc=gs)
        scan(hf("G", X), ge, A("ZR"), ADD, ADD)
        act(A("DC"), A("D2E"), ACT.Identity, scale=gs)
        mm(B(2 + X, 0, 256), M("K5"), A("ONES"))
        mm(B(2 + X, 0, 256), M("D2"), hf("G", X), False)
        mm(B(2 + X, 0, 256), A("DC"), A("ONES"), False)
        tt(hf("U", X), B(2 + X, 0, 256), ge, MUL)
        for s in range(16):
            mm(B(U1, 0, 16), red("RPH", s), cs("U", 256 * X + s, 256 * X + 256, 16), s == 0)
        ts(hf("OT", X, 16), B(U1, 0, 16), float(H - 1), ADD)
        mm(B(U2, 256, 512), red("RP16", 2), cs("W16", 512 * X, 512 * X + 256))
        mm(B(U2, 256, 512), red("RP", 0), rb, False)
        mm(B(U2, 256, 512), A("R1F"), rc, False)
        act(hf("VALS", X), B(U2, 256, 512), ACT.Identity, bias=C("vb"))
        cp(ind(A("CW"), hf("OT", X, 16)), hf("VALS", X))
        copy(hf("CC", X), ind(A("CW"), A("LC")), "CC%d" % X)
        for jh in range(2):
            mm(B(U2, jh, 24, 2), cs("CC", 256 * X + 128 * jh, 256 * X + 128 * jh + 128), cs("SEL", 0, 12))
        if (t, X) != (RO - 1, 1):
            refill()
        obz, obb = cs("OB", 16 * X, 16 * X + 8), cs("OB", 16 * X + 8, 16 * X + 16)
        cp(obb, B(U2, 0, 8))
        ts(hf("OE", X, 128), ind(WN, obb), float(-FL), ADD)
        ts(hf("TS", X, 16), B(U2, 0, 16), float(FL), ADD)
        tt(hf("Z3", X, 8), cs("TS", 16 * X + 8, 16 * X + 16), B(U2, 16, 24), MAX)
        ts(obz, hf("Z3", X, 8), float(-FL), ADD)

    def prepare(X):
        sb = 6 + X
        ob, obb = hf("OB", X, 16), cs("OB", 16 * X + 8, 16 * X + 16)
        prio[0] = PR["xz%d" % X]
        copy(hf("XZB", X), ind(WX, ob), "XZ%d" % X)
        prio[0] = PR["xB" if X else "xe"]
        for i in (2, 3, 0, 1):
            lo = 2048 * X + 512 * i
            copy(cs("XE", lo, lo + 512), ind(WX, cs("OE", lo // 16, lo // 16 + 32)), "XE%d%d" % (X, i))
        prio[0] = PR["pB" if X else "prep"]
        either(lambda: ts(hf("BZ", X), ind(WI, ob), float(FL), ADD),
               lambda: act(hf("BZ", X), ind(WI, ob), ACT.Copy, bias=float(FL)), "BZ%d" % X)
        either(lambda: ts(hf("E32", X, 128), hf("OE", X, 128), float(-O), ADD),
               lambda: act(hf("E32", X, 128), ind(WN, obb), ACT.Copy, bias=float(H)), "E%d" % X)
        either(lambda: ts(hf("NFE", X, 128), hf("E32", X, 128), float(W), EQo),
               lambda: act(hf("NFE", X, 128), hf("E32", X, 128), ACT.Relu, bias=float(1 - W)), "NE%d" % X)
        mm(B(sb, 0, 128), M("I"), cs("XZB", 256 * X, 256 * X + 128))
        mm(B(sb, 0, 128), M("NI"), cs("XZB", 256 * X + 128, 256 * X + 256), False)
        act(hf("M0", X, 128), B(sb, 0, 128), ACT.Abs)
        prio[0] = PR["so%d" % X]
        for h in range(2):
            tt(cs("ED", 256 * X + 128 * h, 256 * X + 128 * h + 128),
               ind(cs("TS", 16 * X, 16 * X + 8), cs("LH", 8 * h, 8 * h + 8)), cs("BZ", 256 * X + 128, 256 * X + 256), EQo)
        scan(hf("DUP", X), hf("ED", X), A("MASK"), MAX, MIN)

    def judge(X, p0, n, parts, acc, qb):
        first = p0 + n == 128
        tag = "%d" % (X if first else 2)
        g0 = 128 * X + p0

        def part(name):
            return cs(name, g0, g0 + n)

        def xzb(z, p, m):
            return cs("XZB", 256 * X + 128 * z + p, 256 * X + 128 * z + p + m)
        prio[0] = PR["pat" + tag]
        mm(B(acc, 0, n), M("NBD"), xzb(0, p0, n))
        if first:
            prio[0] = PR["so%d" % X]
            mm(B(acc, 256, 264), A("I32M"), cs("TS", 16 * X, 16 * X + 8), False)
            for h in range(2):
                e0 = 256 * X + 128 * h
                mm(B(acc, 256 + h, 264, 2), M("IB"), cs("DUP", e0 + 31, e0 + 128, 32), False)
        prio[0] = PR["sum" + tag]
        mm(B(acc, n, 2 * n), M("NBD"), xzb(0, p0, n), False)
        for ih in range(2):
            reg = B(acc, n * ih, n * ih + n)
            mm(reg, M("NHI"), part("M0"), False)
            mm(reg, M("N%d" % ih), part("NFE"), False)
        for p, nmax, pz, pb, spare in parts:
            dif = (pb, spare) if nmax == 0 else (spare,)
            lo, hi = 2048 * X + 16 * p, 2048 * X + 16 * p + 1024
            xz, xb = xzb(0, p, 64), xzb(1, p, 64)
            prio[0] = PR["pat" + tag]
            for bank, x in ((pz, xz), (pb, xb))[:2 if nmax else 1]:
                for i in range(8):
                    mm(B(bank, i, 512, 8), M("I"), x)
            prio[0] = PR["sum" + tag]
            for ih in range(2 if nmax else 0):
                mm(B(acc, n * ih + p - p0, n * ih + p - p0 + 64), M("LO%d" % (2 - nmax)), xb, False)
            for q in range(2):
                bymax = q < nmax
                xe = cs("XE", lo + q, hi, 2)
                ks = range(q, 16, 2)
                regs = [B(acc, n * (k // 8) + p - p0, n * (k // 8) + p - p0 + 64) for k in ks]
                prio[0] = PR["je" + tag]
                for j, k in enumerate(ks):
                    mm(regs[j], red("JE", 8 + k % 8) if bymax else red("JE2", k % 8), cs("XE", lo + k, hi, 16), False)
                for z in range(2):
                    m0 = V * (ring[1] % 8)
                    ring[1] += 1
                    prio[0] = PR["max" + tag]
                    if z == 0 or bymax:
                        tt(cs("MM", m0, m0 + V), xe, B(pb if z else pz), MAX)
                    else:
                        prio[0] = PR["dif" + tag]
                        d = dif[q % len(dif)]
                        mm(B(d), M("I"), xe)
                        for i in range(8):
                            mm(B(d, i, 512, 8), M("NI"), xb, False)
                        act(cs("MM", m0, m0 + V), B(d), ACT.Abs)
                    prio[0] = PR["sum" + tag]
                    for j, k in enumerate(ks):
                        mm(regs[j], red("JZ" if z == 0 else "JB" if bymax else "JE", k % 8), cs("MM", m0 + j, m0 + V, 8), False)
        o1, o2 = B(qb, 0, n), B(qb, n, 2 * n)
        prio[0] = PR["fin" + tag]
        mm(o1, M("I"), cs("BZ", 256 * X + p0, 256 * X + p0 + n))
        mm(o1, M("NO"), cs("ONES", 0, n), False)
        mm(o1, M("TA0"), part("NFE"), False)
        ts(cs("FF", 2 * g0, 2 * g0 + 2 * n), B(acc, 0, 2 * n), 0.0, LT)
        if first:
            tt(hf("SO1", X, 8), B(acc, 256, 264), A("DJ"), MIN)
            ts(hf("SO", X, 8), hf("SO1", X, 8), C("xo"), ADD)
        for ih in range(2):
            mm(o1, M("M2%d" % ih), cs("FF", 2 * g0 + n * ih, 2 * g0 + n * ih + n), False)
        for ih in range(2):
            mm(o2, M("M1%d" % ih), cs("FF", 2 * g0 + n * ih, 2 * g0 + n * ih + n), ih == 0)
        tt(part("G1"), part("E32"), o2, MAX)
        tt(part("NEW"), part("G1"), o1, MIN)
        for q in reversed(range(g0 // 32, (g0 + n) // 32)):
            cp(ind(A("P32"), cs("SO", 2 * q, 2 * q + 2)), cs("NEW", 32 * q, 32 * q + 32))

    for t in range(RO):
        window(t)
        complaints(0)
        mark["g0"], mark["g1"] = gat[-len(GL[0])], gat[1 - len(GL[0])]
        for a, b in (FIRST if t else FIRST0):
            ops[mark[b]]["after"].add(mark[a])
        middle(t, 0)
        prepare(0)
        if t == 0:
            prio[0] = 4
            aff(cs("P32", 0, V), A("P16"), 1, H)
            ops[-1]["after"].add(gat[-1])
        complaints(1)
        middle(t, 1)
        judge(0, 0, 128, [(64, NMAX[0], 4, 5, 6), (0, NMAX[1], 4, 5, 6)], 2, 6)
        prepare(1)
        judge(1, 64, 64, [(64, NMAX[2], 0, 1, 7)], 3, 7)
        judge(1, 0, 64, [(0, NMAX[3], 4, 5, 6)], 2, 6)

    prio[0] = 0
    dma("s", A("YS"), cs("P32", 0, V), "ys")
    dma("a", A("y", slice(16 * R, 16 * R + 16), al), A("P32", slice(16 * R, 16 * R + 16), slice(0, V)), "yo")
    send(lambda q: A("YS", q), A("YR", R), "ya%d" % R)
    for i, q in enumerate(others):
        arrive(q, A("YR", q), "ya%d" % q, 1000.0)
        dma("s" if i % 2 == 0 else "a", A("y", slice(16 * q, 16 * q + 16), al), A("YR", q), "yo")

    bysem = {}
    for i, o in enumerate(ops):
        if o["sem"] is not None:
            bysem.setdefault(o["sem"], []).append(i)
    users = [[] for _ in ops]
    for i, o in enumerate(ops):
        o["pre"] = set(o["after"])
        for d in o["deps"]:
            o["pre"].update(bysem[ops[d]["sem"]] if ops[d]["sem"] is not None else [d])
        o["left"], o["ready"], o["tail"] = len(o["pre"]), 0.0, 0.0
        for d in o["pre"]:
            users[d].append(i)
    for _ in range(2):
        for i in reversed(range(len(ops))):
            o = ops[i]
            c = min(o["cost"].values()) if o["eng"] == "?" else min(o["cost"], 20.0)
            o["tail"] = c + max([0.0] + [ops[u]["tail"] + 0.1 for u in users[i]])
    free = {e: 0.0 for e in list(queue) + ["x"]}
    ready = {e: [] for e in free}

    def offer(i):
        for e in ("va" if ops[i]["eng"] == "?" else ops[i]["eng"]):
            ready[e].append(i)

    def rank(j, e):
        o = ops[j]
        return (o["prio"] + (SHY if o["eng"] == "?" and e == "v" else 0) - TAILW * o["tail"], j)

    for i, o in enumerate(ops):
        if o["left"] == 0:
            offer(i)
    order = []
    while len(order) < len(ops):
        best = None
        for e in ("x", "s", "g", "t", "a", "v"):
            if ready[e]:
                now = max(free[e], min(ops[i]["ready"] for i in ready[e]))
                i = min((j for j in ready[e] if ops[j]["ready"] <= now + SLACK), key=lambda j: rank(j, e))
                start = max(free[e], ops[i]["ready"])
                if best is None or start < best[0]:
                    best = (start, i, e)
        start, i, e = best
        o = ops[i]
        if o["eng"] == "?":
            ready["a" if e == "v" else "v"].remove(i)
            o["eng"], o["call"], o["cost"], o["hold"] = e, o["call"][e], o["cost"][e], o["cost"][e]
        ready[e].remove(i)
        o["pos"] = len(order)
        order.append(i)
        if e != "x":
            free[e] = start + o["hold"]
        for u in users[i]:
            p = ops[u]
            gap = 0.0 if i in p["after"] and i not in p["deps"] else o["cost"] + 0.1
            p["ready"] = max(p["ready"], start + gap)
            p["left"] -= 1
            if p["left"] == 0:
                offer(u)

    for o in ops:
        latest = {}
        for d in o["deps"]:
            e = ops[d]["eng"]
            if ops[d]["sem"] is None and (e not in latest or ops[d]["pos"] > ops[latest[e]]["pos"]):
                latest[e] = d
        o["deps"] = [d for d in o["deps"] if ops[d]["sem"] is not None] + list(latest.values())
        for d in o["deps"]:
            ops[d]["sig"] = True
    done = {}
    for i in order:
        o = ops[i]
        if o["sem"] is None and o["sig"]:
            done[o["eng"]] = done.get(o["eng"], 0) + 1
            o["n"] = done[o["eng"]]
    seen = {}
    for i in order:
        o = ops[i]
        if o["eng"] == "x":
            continue
        need = {}
        for d in o["deps"]:
            p = ops[d]
            s, v = (p["sem"], total[p["sem"]]) if p["sem"] is not None else (csem[p["eng"]], p["n"])
            need[s] = max(need.get(s, 0), v)
        for s in sorted(need):
            if seen.get((o["eng"], s), 0) < need[s]:
                queue[o["eng"]].wait_ge(T.sem[s], need[s])
                seen[(o["eng"], s)] = need[s]
        r = o["call"]()
        if o["sem"] is None and o["sig"]:
            r.then_inc(T.sem[csem[o["eng"]]], 1)
    for e in done:
        total[csem[e]] = done[e]
    for s in sorted(total):
        if max([seen.get((e, s), 0) for e in queue]) < total[s]:
            g.wait_ge(T.sem[s], total[s])
